import numpy as np, ml_dtypes
CORES = [3,7,11,15,131,135,139,143]
N = 8
import mx_ref
BF = ml_dtypes.bfloat16
def entries(a):
    return np.ascontiguousarray(a.T).reshape(-1)
def table(e):
    return np.ascontiguousarray(np.reshape(e, (-1, 16)).T).astype(np.int32)
def pick(q, e):
    c = np.concatenate([q[0].reshape(128, -1, 4), np.zeros((128, 1, 4), np.uint8)], axis=1); s = np.concatenate([q[1], np.ones((16, 1), np.uint8)], axis=1)
    return (np.ascontiguousarray(c[:, e].reshape(128, -1)), np.ascontiguousarray(s[:, e]))
def join(*qs):
    return (np.concatenate([q[0] for q in qs], axis=1), np.concatenate([q[1] for q in qs], axis=1))
def put(q, e, v):
    c, s = q[0].reshape(128, -1, 4).copy(), q[1].copy(); c[:, e] = v[0].reshape(128, -1, 4); s[:, e] = v[1]
    return (c.reshape(128, -1), s)
def pk(c, s):
    return (np.ascontiguousarray(c), mx_ref.live(s))
def emit(q):
    return q[0], q[1]
def decode(q):
    o = []
    for b in range(4):
        e = np.zeros((128, 128, 4), np.float32); e[np.arange(128), np.arange(128), b] = 1
        o.append(mx_ref.matmul(mx_ref.quantize(e.reshape(128, 512).astype(BF)), q))
    return np.stack(o, axis=2).reshape(128, -1)
def f(rng, *shape):
    return mx_ref.flush((rng.standard_normal(shape, dtype=np.float32) * np.exp2(rng.integers(-2, 3, shape[:-1] + (1,)))).astype(BF))
def wide(rng, *shape, cols=0):
    v = rng.standard_normal(shape, dtype=np.float32) * np.exp2(rng.integers(-12, 13, shape)).astype(np.float32)
    if cols: v *= np.repeat(np.exp2(rng.integers(-cols, cols + 1, shape[:-2] + (1, shape[-1] // 4))) * (rng.random(shape[:-2] + (1, shape[-1] // 4)) > 0.0625), 4, axis=-1).astype(np.float32)
    return mx_ref.flush(v.astype(BF))
P, F, R = 128, 16, 2
def big(v):
    v = np.array(v, np.float32)
    v[np.abs(v) < np.float32(2.0 ** -16)] = 0
    return v.astype(BF)
def share(v):
    return big(np.ascontiguousarray(v.reshape(128, N, 4 * P).transpose(1, 0, 2)))
def links(nb):
    return np.concatenate([entries(nb[r]).reshape(P, 3) for r in range(N)])
def graph(rng, ends=False):
    to, far, n = np.zeros((N * P, 3), int), [], P - (N - 1) * F
    for r in range(N):
        a, i = P * r + rng.permutation(P), 0
        while i < P:
            m = min(2 * int(rng.integers(2, 17)), P - i)
            if P - i - m < 4: m = P - i
            for k in range(2):
                c = np.roll(a[i:i + m], -k)
                to[c[0::2], k], to[c[1::2], k] = c[1::2], c[0::2]
            i += m
        if ends:
            h = rng.permutation(a[a < to[a, 0]])[:n]
            e = np.where(rng.random(n) < 0.5, h, to[h, 0])
        else: e = rng.permutation(a)[:n]
        far.append(rng.permutation(np.setdiff1d(a, e)).reshape(N - 1, F))
        for i in range(0, n, 2):
            if e[i + 1] in to[e[i], :2]:
                for j in range(0, n, 2):
                    if j != i and e[j + 1] not in to[e[i], :2] and e[i + 1] not in to[e[j], :2]:
                        e[i + 1], e[j + 1] = e[j + 1], e[i + 1]
                        break
        to[e[0::2], 2], to[e[1::2], 2] = e[1::2], e[0::2]
    for r in range(N):
        for q in range(r + 1, N):
            u, v = far[r][q - 1], far[q][r]
            to[u, 2], to[v, 2] = v, u
    return to
def inputs(rng, x, to):
    return {"x": x, "nb": np.stack([table(to[P * r:P * r + P].reshape(-1)) for r in range(N)]), "w": f(rng, N, 128, 512)}
def setup_inputs(rng):
    return inputs(rng, big(f(rng, N, 128, 4 * P)), graph(rng))
def setup_inputs_far(rng):
    to, n = graph(rng), np.arange(N * P)
    v = (1 + 0.5 * rng.random((128, N * P, 4))) * rng.choice([-1.0, 1.0], (128, N * P, 4))
    a = n[(to[:, 2] // P != n // P) & (n < to[:, 2])]
    b = to[a, 2]
    v[:, b] = np.abs(v[:, b]) * np.sign(v[:, a]) * np.where(rng.random((128, a.size, 4)) < 0.125, -1.0, 1.0)
    return inputs(rng, share(v), to)
def setup_inputs_none(rng):
    to, n, z = graph(rng, ends=True), np.arange(N * P), int(rng.integers(0, N))
    own = n // P == z
    size = np.where(own & (to[:, 2] // P == z), 0.125, 1.0)
    color = np.full(N * P, -1)
    for a in n[n < to[:, 0]]:
        both = np.array([a, to[a, 0]])
        near = color[to[both, 1:]].reshape(-1).tolist()
        color[both] = next(int(c) for c in rng.permutation(5) if c not in near)
    v = rng.choice([-1.0, 1.0], (128, N * P, 4))
    a = n[(to[:, 2] // P != n // P) & (n < to[:, 2])]
    v[:, to[a, 2]] = v[:, a]
    v[:40] = np.where((np.arange(40) // 8)[:, None, None] == color[None, :, None], 8.0, 0.0)
    v[40:48] = 64.0
    v = np.where(own[None, :, None], (1 + 0.5 * rng.random((128, N * P, 4))) * size[None, :, None], 16.0 * v)
    return inputs(rng, share(v), to)
def setup_inputs_spread(rng):
    return inputs(rng, big(wide(rng, N, 128, 4 * P, cols=6)), graph(rng))
def setup_inputs_ties(rng):
    to = graph(rng)
    t = f(rng, 128, 12).astype(np.float32).reshape(128, 3, 4)
    five = np.concatenate([t, 0 - t[:, :1], np.zeros((128, 1, 4), np.float32)], axis=1)
    e = rng.integers(0, 5, N * P)
    for r in range(N):
        j = P * r + int(rng.integers(0, P))
        e[to[j]] = 0
        e[to[to[j]].reshape(-1)] = 0
    return inputs(rng, share(five[:, e]), to)
def setup_inputs_twice(rng):
    to, large = graph(rng), np.zeros(N * P, bool)
    v = np.abs(rng.standard_normal((128, N * P, 4))) * np.exp2(rng.integers(-1, 2, (1, N * P, 1)))
    for i in range(P // 32):
        for r in rng.permutation(N):
            for j in rng.permutation(P):
                n1 = P * r + j
                n2 = to[n1, 1]
                p = np.array([to[n1, 0], n1, n2, to[n2, 0]])
                if i == 0:
                    m = to[[n1, n2], 2]
                    q = np.concatenate([p, m])
                    if large[q].any() or large[to[q]].any() or np.count_nonzero(np.isin(to[q], q)) != 10: continue
                    size = np.concatenate([rng.choice([1.0, 1.25], (128, 4, 4)), rng.choice([3.5, 4.0], (128, 2, 4))], axis=1) * 2.0 ** 26
                    v[:, q] = size * rng.choice([-1.0, 1.0], (128, 1, 4)) * np.array([1.0, 1.0, -1.0, -1.0, -1.0, 1.0])[None, :, None]
                    large[q] = True
                    large[to[m]] = True
                    break
                if large[p].any() or large[to[p]].any() or np.isin(to[p, 2], p).any() or to[p[0], 1] == p[3]: continue
                large[p] = True
                v[:, p] = (1 + 0.5 * rng.random((128, 4, 4))) * np.array([256.0, 64.0, 64.0, 256.0])[None, :, None]
                break
    return inputs(rng, share(v), to)
def check_inputs(d):
    b = []
    for k, low, high in (("x", -16, 28), ("w", -30, 30)):
        v = np.abs(d[k].astype(np.float32))
        if not (np.isfinite(v).all() and ((v == 0) | (v >= 2.0 ** low) & (v <= 2.0 ** high)).all()): b.append("a value of " + k)
    to, n = links(d["nb"]), np.arange(N * P)
    if to.min() < 0 or to.max() >= N * P: return b + ["range of nb"]
    for k in range(3):
        if (to[to[:, k], k] != n).any() or (to[:, k] == n).any(): b.append("edges k = %d are no pairs" % k)
    if (to[:, :2] // P != n[:, None] // P).any(): b.append("an edge k = 0 or 1 leaves its rank")
    if (to[:, 0] == to[:, 1]).any() or (to[:, 0] == to[:, 2]).any() or (to[:, 1] == to[:, 2]).any(): b.append("two edges of a node lead to the same node")
    c = np.zeros((N, N), int)
    np.add.at(c, (n // P, to[:, 2] // P), 1)
    if (c[~np.eye(N, dtype=bool)] != F).any(): b.append("number of edges between two ranks")
    return b
def scores(h, to):
    s = np.zeros((N * P, 3), np.float32)
    for i in range(0, N * P, 128):
        a = pick(h, np.arange(i, i + 128))
        for k in range(3): s[i:i + 128, k] = np.diagonal(mx_ref.matmul(a, pick(h, to[i:i + 128, k]))) + np.float32(0)
    return s
def reference(x, nb, w):
    to, n = links(nb), np.arange(N * P)
    h = join(*[mx_ref.quantize(np.ascontiguousarray(x[r])) for r in range(N)])
    merged, pr = np.zeros((N * P, 3), bool), np.zeros((N, R, P), np.float32)
    for t in range(R):
        s = scores(h, to)
        s[merged] = -np.inf
        c = np.argmax(s, axis=1)
        v = to[n, c]
        met = c[v] == c
        merged[n[met], c[met]] = True
        pr[:, t] = np.where(met, v, -1).reshape(N, P)
        d = decode(h).reshape(128, N * P, 4)
        m = np.float32(0.5) * d + np.float32(0.5) * d[:, np.where(met, v, n)]
        new = mx_ref.quantize(np.ascontiguousarray(m.reshape(128, -1).astype(BF)))
        h = pick(join(h, new), np.where(met, N * P + n, n))
    oc, osc, y = np.zeros((N, 128, 4 * P), np.uint8), np.zeros((N, 16, P), np.uint8), np.zeros((N, 128, P), np.float32)
    for r in range(N):
        own = pick(h, np.arange(P * r, P * r + P))
        oc[r], osc[r] = emit(own)
        y[r] = mx_ref.matmul(mx_ref.quantize(np.ascontiguousarray(w[r])), own)
    return {"oc": oc, "osc": osc, "pr": pr, "y": y}

@@ -1,0 +1,458 @@
+from concourse.bass import DstId, RemoteDMATransfer
+from concourse.mybir import dt, AluOpType as OP, AxisListType, ActivationFunctionType as AF
+
+F32, BF16, I32, U16, U8, C4 = "float32", "bfloat16", "int32", "uint16", "uint8", "float8_e4m3fn_x4"
+
+SCRATCH = {
+    "nbt": ("sbuf", [128, 3], I32), "nbr": ("sbuf", [128, 384], I32), "nbb": ("sbuf", [128, 384], I32),
+    "xt": ("sbuf", [128, 512], BF16), "wt": ("sbuf", [128, 512], BF16),
+    "icol": ("sbuf", [128, 32], I32), "fcol": ("sbuf", [128, 64], F32),
+    "cc3": ("sbuf", [128, 4], F32), "d8": ("sbuf", [128, 8], F32), "mk2": ("sbuf", [128, 4], F32), "dm": ("sbuf", [128, 8], F32),
+    "wts": ("sbuf", [128, 4], F32),
+    "npi": ("sbuf", [128, 128], I32), "npa": ("sbuf", [128, 128], I32), "npf": ("sbuf", [128, 128], F32), "ir": ("sbuf", [128, 128], F32),
+    "ones": ("sbuf", [128, 128], F32), "k128": ("sbuf", [128, 128], F32), "wm": ("sbuf", [128, 128], F32), "sm": ("sbuf", [128, 128], F32),
+    "eye": ("sbuf", [128, 128], F32), "ks": ("sbuf", [128, 512], F32),
+    "et": ("sbuf", [128, 520], BF16), "eq": ("sbuf", [128, 512], C4), "es": ("sbuf", [128, 512], U8),
+    "swl": ("sbuf", [128, 2], U16),
+    "n2m": ("sbuf", [128, 4], I32),
+    "zk": ("sbuf", [128, 128], F32), "rk": ("sbuf", [128, 128], F32), "sgn": ("sbuf", [128, 128], BF16),
+    "zx": ("sbuf", [128, 128], F32), "rx": ("sbuf", [128, 128], F32), "dx": ("sbuf", [128, 128], F32),
+    "pl": ("sbuf", [128, 8], U16), "tli": ("sbuf", [128, 24], I32), "tla": ("sbuf", [128, 24], I32), "tlb": ("sbuf", [128, 24], I32),
+    "tlc": ("sbuf", [128, 24], I32), "tl": ("sbuf", [128, 24], U16),
+    "prw": ("sbuf", [128, 512], F32), "e0": ("sbuf", [128, 128], BF16), "e1": ("sbuf", [128, 128], BF16),
+    "lm": ("sbuf", [128, 256], F32), "lpi": ("sbuf", [128, 8], I32), "lpa": ("sbuf", [128, 8], I32), "lpb": ("sbuf", [128, 8], I32), "ll": ("sbuf", [128, 16], U16),
+    "posr": ("sbuf", [128, 128], F32), "posm": ("sbuf", [128, 128], F32), "poss": ("sbuf", [128, 128], F32), "pol": ("sbuf", [128, 8], U16),
+    "selr": ("sbuf", [128, 128], F32), "selm": ("sbuf", [128, 256], F32),
+    "q0": ("sbuf", [128, 128], C4), "q0s": ("sbuf", [128, 128], U8),
+    "wq": ("sbuf", [128, 128], C4), "wqs": ("sbuf", [128, 128], U8),
+    "f0": ("sbuf", [128, 128], C4), "f0s": ("sbuf", [128, 128], U8), "f1": ("sbuf", [128, 128], C4), "f1s": ("sbuf", [128, 128], U8),
+    "yo": ("sbuf", [128, 128], F32),
+    "pn": ("psum", [128, 2048], F32), "pm": ("psum", [128, 2048], F32),
+}
+for _c in ("p", "l", "v0", "v1"):
+    SCRATCH["qz" + _c] = ("sbuf", [128, 128], F32)
+    SCRATCH["qt" + _c] = ("sbuf", [128, 128], F32)
+    SCRATCH["qs" + _c] = ("sbuf", [128, 128], F32)
+for _t in "01":
+    SCRATCH.update({
+        "w" + _t: ("sbuf", [128, 512], C4), "ws" + _t: ("sbuf", [128, 512], U8),
+        "g" + _t: ("sbuf", [128, 256], C4), "gs" + _t: ("sbuf", [128, 256], U8),
+        "land" + _t: ("sbuf", [128, 128], C4), "lands" + _t: ("sbuf", [128, 128], U8),
+        "lt" + _t: ("sbuf", [128, 8], F32), "tq" + _t: ("sbuf", [128, 8], F32),
+        "mb" + _t: ("sbuf", [128, 32], F32), "mx" + _t: ("sbuf", [128, 32], F32), "my" + _t: ("sbuf", [128, 32], F32), "mz" + _t: ("sbuf", [128, 32], F32),
+        "sc" + _t: ("sbuf", [128, 32], F32), "pen" + _t: ("sbuf", [128, 8], F32), "met" + _t: ("sbuf", [128, 4], F32), "mew" + _t: ("sbuf", [128, 4], F32),
+        "ex" + _t: ("sbuf", [128, 1024], F32), "nt" + _t: ("sbuf", [128, 1536], BF16),
+        "vl" + _t: ("sbuf", [128, 8], U16), "prs" + _t: ("sbuf", [128, 128], F32), "pro" + _t: ("sbuf", [128, 128], F32),
+    })
+DMAS = ["d_nbt", "d_nbr", "d_x", "d_w", "d_oc", "d_os0", "d_os1", "d_os2", "d_os3", "d_y", "d_p0", "d_p1"]
+SEMAPHORES = ["cV", "cS", "cT", "cG", "sent", "arr0", "arr1", "thr0", "thr1"] + DMAS
+BIG = 1e29
+
+
+def rank_program(g, core, T, topo):
+    r = T.rank_of(core)
+    if r is None:
+        return
+    N, cores = len(T.cores), T.cores
+    queue = {"V": g.vector, "S": g.scalar, "T": g.tensor, "G": g, "Y": g.sync}
+    count = {e: 0 for e in "VSTG"}
+    known = {e: {} for e in "VSTGY"}
+    snap, hist, waited, total = {}, {}, {}, {}
+
+    def v(name, c0=0, c1=None, st=1, p0=0, p1=128):
+        c1 = SCRATCH[name][1][1] if c1 is None else c1
+        ap = T[name][p0:p1, c0:c1] if st == 1 else T[name][p0:p1, c0:c1:st]
+        if SCRATCH[name][0] == "psum":
+            return (ap, name, 0, 128, c0 // 512 * 512, (c1 + 511) // 512 * 512, 1)
+        return (ap, name, p0, p1, c0, c1, st)
+
+    def meet(a, b):
+        if a[3] <= b[2] or b[3] <= a[2] or a[5] <= b[4] or b[5] <= a[4]:
+            return False
+        return not (a[6] == b[6] and a[6] > 1 and (a[4] - b[4]) % a[6])
+
+    def need(e, tok):
+        sem, val = tok
+        if known[e].get(sem, 0) < val:
+            queue[e].wait_ge(T.sem[sem], val)
+            waited[sem] = max(waited.get(sem, 0), val)
+            for s, n in list(snap.get(tok, {}).items()) + [(sem, val)]:
+                known[e][s] = max(known[e].get(s, 0), n)
+
+    def order(e, outs, ins):
+        for x in ins:
+            psum = SCRATCH[x[1]][0] == "psum"
+            for (y, tok, w, f) in hist.get(x[1], []):
+                if (w or (psum and f != e)) and meet(x, y):
+                    need(e, tok)
+        for x in outs:
+            for (y, tok, w, f) in hist.get(x[1], []):
+                if (f != e or e != "T") and meet(x, y):
+                    need(e, tok)
+
+    def note(e, outs, ins, tok):
+        for x in outs:
+            hist.setdefault(x[1], []).append((x, tok, True, e))
+        for x in ins:
+            hist.setdefault(x[1], []).append((x, tok, False, e))
+
+    def run(e, outs, ins, call):
+        outs = [x for x in outs if isinstance(x, tuple)]
+        ins = [x for x in ins if isinstance(x, tuple)]
+        order(e, outs, ins)
+        count[e] += 1
+        tok = ("c" + e, count[e])
+        call().then_inc(T.sem[tok[0]], 1)
+        total[tok[0]] = count[e]
+        snap[tok] = dict(known[e])
+        note(e, outs, ins, tok)
+
+    def val(x):
+        return x[0] if isinstance(x, tuple) else x
+
+    def dma(e, sem, out, in_):
+        outs, ins = [x for x in (out,) if isinstance(x, tuple)], [x for x in (in_,) if isinstance(x, tuple)]
+        order(e, outs, ins)
+        queue[e].dma_start(val(out), val(in_)).then_inc(T.sem[sem], 16)
+        total[sem] = 16
+        snap[(sem, 16)] = dict(known[e])
+        note("D" + sem, outs, ins, (sem, 16))
+
+    def ts(out, a, s1, op0, s2=None, op1=None):
+        if op1 is None:
+            run("V", [out], [a, s1], lambda: g.vector.tensor_scalar(out[0], a[0], val(s1), None, op0))
+        else:
+            run("V", [out], [a, s1, s2], lambda: g.vector.tensor_scalar(out[0], a[0], val(s1), val(s2), op0, op1))
+
+    def tt(out, a, b, op):
+        run("V", [out], [a, b], lambda: g.vector.tensor_tensor(out[0], a[0], b[0], op))
+
+    def cp(out, a, e="V"):
+        if e == "V":
+            run("V", [out], [a], lambda: g.vector.tensor_copy(out[0], a[0]))
+        else:
+            run("S", [out], [a], lambda: g.scalar.activation(out[0], a[0], AF.Copy))
+
+    def fill(out, c):
+        run("V", [out], [], lambda: g.vector.memset(out[0], c))
+
+    def red(out, a, op, ab=False):
+        run("V", [out], [a], lambda: g.vector.tensor_reduce(out[0], a[0], AxisListType.X, op, apply_absolute_value=ab))
+
+    def total_s(out, a, bias=None):
+        if bias is None:
+            run("S", [out, a], [a], lambda: g.scalar.activation(a[0], a[0], AF.Copy, accum_out=out[0]))
+        else:
+            run("S", [out, a], [a, bias], lambda: g.scalar.activation(a[0], a[0], AF.Identity, bias=bias[0], accum_out=out[0]))
+
+    def turn(out, a):
+        run("V", [out], [a], lambda: g.vector.transpose(out[0], a[0]))
+
+    def scan(z, q):
+        s = v("sm")
+        run("V", [z], [q, s], lambda: g.vector.tensor_tensor_scan(z[0], s[0], q[0], 0.0, OP.mult, OP.add))
+
+    def quant(q, s, a):
+        run("V", [q, s], [a], lambda: g.vector.quantize_mx(q[0], s[0], a[0]))
+
+    def mm(out, a, asc, b, bsc, start=True, stop=True):
+        run("T", [out], [a, asc, b, bsc], lambda: g.tensor.matmul_mx(out[0], a[0], asc[0], b[0], bsc[0], start, stop))
+
+    def gather(out, win, off, e="V"):
+        run(e, [out], [win, off], (lambda: g.vector.tensor_copy(out[0], win[0].indirect(off[0]))) if e == "V"
+            else (lambda: g.scalar.activation(out[0], win[0].indirect(off[0]), AF.Copy)))
+
+    def pick(oq, os, oa, ob, iq, isc, ia, ib, off):
+        o, w = v(oq, oa, ob), v(iq, ia, ib)
+        run("V", [o], [w, off], lambda: g.vector.tensor_copy(o[0].bitcast(dt.uint32), w[0].bitcast(dt.uint32).indirect(off[0])))
+        gather(v(os, oa, ob), v(isc, ia, ib), off, "S")
+
+    def iota(out, pattern, base, cm, flag):
+        run("G", [out], [], lambda: g.iota(out[0], pattern, base, cm, allow_small_or_imprecise_dtypes=True) if flag else g.iota(out[0], pattern, base, cm))
+
+    def quarters(name, c0, st):
+        for e, d in (("V", 0), ("S", 1), ("V", 2), ("S", 3)):
+            a = d ^ 1
+            cp(v(name, 32 * a + c0, 32 * a + 32, st, 32 * d, 32 * d + 32), v(name, 32 * a + c0, 32 * a + 32, st, 32 * a, 32 * a + 32), e)
+        cp(v(name, 64 + c0, 128, st, 0, 64), v(name, 64 + c0, 128, st, 64, 128), "V")
+        cp(v(name, c0, 64, st, 64, 128), v(name, c0, 64, st, 0, 64), "S")
+
+    def wrap(tag, col):
+        ts(v("qz" + tag), v("wm"), col, OP.mult)
+        turn(v("qt" + tag), v("qz" + tag))
+        scan(v("qs" + tag), v("qt" + tag))
+        quarters("qs" + tag, 15, 16)
+        return v("qs" + tag, 15, 128, 16)
+
+    def ic(k):
+        return v("icol", k, k + 1)
+
+    def fc(k):
+        return v("fcol", k, k + 1)
+
+    dma("Y", "d_nbt", v("nbt"), T.nb[:, :])
+    dma("S", "d_x", v("xt"), T.x[:, :])
+    dma("Y", "d_nbr", v("nbr", 0, 384, 1, 0, 1), T.nb[:, :])
+    dma("Y", "d_w", v("wt"), T.w[:, :])
+
+    iota(ic(0), [[0, 1]], 0, 1, False)
+    iota(v("cc3", 0, 3), [[1, 3]], 0, 0, True)
+    iota(v("npi"), [[1, 128]], 128, -1, False)
+    fill(v("ones"), 1.0)
+    fill(v("k128"), 128.0)
+    fill(v("sm"), 1.0)
+    ts(ic(1), ic(0), 3, OP.arith_shift_right)
+    ts(ic(2), ic(0), 7, OP.bitwise_and)
+    ts(ic(6), ic(0), 16 * r, OP.bitwise_and)
+    cp(fc(3), ic(0))
+    ts(ic(3), ic(1), 11, OP.mult)
+    ts(fc(0), ic(1), -5, OP.mult, 10, OP.add)
+    ts(fc(1), ic(1), -1, OP.mult, 2, OP.add)
+    ts(ic(4), ic(3), 5, OP.arith_shift_right)
+    ts(fc(4), ic(6), -2, OP.mult, fc(3), OP.add)
+    tt(ic(5), ic(2), ic(4), OP.add)
+    ts(fc(2), ic(4), 3, OP.mult, fc(1), OP.add)
+    ts(v("mk2", 0, 3), v("cc3", 0, 3), fc(2), OP.is_equal)
+    ts(fc(5), ic(5), 16, OP.mult, fc(0), OP.add)
+    ts(fc(6), fc(5), 128 * r, OP.add)
+    ts(fc(7), fc(5), 128 * 127, OP.add)
+    ts(fc(8), fc(4), 16 * r, OP.add, 256, OP.mult)
+    ts(v("npa"), v("npi"), 15, OP.bitwise_and)
+    fill(v("sm", 0, 128, 16), 0.0)
+    ts(v("wm"), v("npa"), 0, OP.is_equal)
+
+    tt(v("n2m", 0, 3), v("nbt"), v("mk2", 0, 3), OP.mult)
+    red(ic(8), v("n2m", 0, 3), OP.max)
+    ts(ic(9), ic(8), 896, OP.bitwise_and)
+    ts(fc(9), ic(8), 0.5, OP.add, fc(6), OP.min)
+    ts(fc(10), ic(9), 8, OP.mult, fc(9), OP.add)
+    ts(v("zk"), v("ones"), fc(10), OP.mult)
+    turn(v("rk"), v("zk"))
+    quarters("rk", 0, 1)
+    kk, kb, sg, ac = v("rk"), fc(10), v("sgn"), fc(11)
+    run("S", [sg, ac], [kk, kb], lambda: g.scalar.activation(sg[0], kk[0], AF.Sign, bias=kb[0], scale=-1.0, accum_out=ac[0]))
+    iota(v("ir"), [[1, 128]], 0, 0, True)
+    nb1, nball = v("nbr", 0, 384, 1, 0, 1), v("nbb")
+    run("G", [nball], [nb1], lambda: g.partition_broadcast(nball[0], nb1[0], 128))
+    iota(v("npf"), [[1, 128]], 0, -1, True)
+    iota(v("d8"), [[1, 8]], 0, 0, True)
+    iota(v("ks"), [[1, 4], [0, 128]], 0, 0, True)
+    ts(v("zx"), v("k128"), fc(11), OP.mult, fc(7), OP.add)
+    turn(v("rx"), v("zx"))
+    quarters("rx", 0, 1)
+    ts(v("dx"), v("rx"), fc(8), OP.subtract)
+    red(fc(12), v("dx"), OP.min, True)
+    wp = wrap("p", fc(12))
+    cp(v("pl"), wp)
+    quant(v("q0"), v("q0s"), v("xt"))
+    pick("w0", "ws0", 0, 128, "q0", "q0s", 0, 128, v("pl"))
+
+    peers = [(d, cores[r ^ d]) for d in range(1, N)]
+    chip = topo.cores_of(core)
+    far = [(d, c) for d, c in peers if c not in chip]
+    near = [(d, c) for d, c in peers if c in chip]
+    lanes = topo.engines(core, far[0][1])
+    ways = {}
+    for k, (d, c) in enumerate(far):
+        ways[d] = [lanes[k]]
+    rest = lanes[len(far):]
+    for k, (d, c) in enumerate(near):
+        ways[d] = rest[k::len(near)]
+    arrive = sum(len(x) for x in ways.values())
+
+    def bits(es):
+        return sum(1 << e for e in es)
+
+    def dest(c):
+        rid, pid = topo.addr(c, core)
+        return DstId(rid=rid, pnc=pid)
+
+    def send(t, part):
+        name, dst = (("w" + t, "land" + t), ("ws" + t, "lands" + t))[part]
+        order("G", [], [v(name, 16, 128)])
+        tr = []
+        for d, c in peers:
+            a, b = T[name][:, 16 * d:16 * d + 16], T[dst][:, 16 * d:16 * d + 16]
+            if part == 0:
+                a, b = a.bitcast(dt.uint8), b.bitcast(dt.uint8)
+            tr.append(RemoteDMATransfer(dst_ids=[dest(c)], dma_engine_mask=bits(ways[d]), remote_sem=T.sem["arr" + t], src=a, dst=b))
+        g.remote_dma_fused(tr, local_sem=T.sem.sent)
+        total["sent"] = total.get("sent", 0) + arrive
+
+    def send_best(t):
+        order("G", [], [v("mb" + t, 0, 1)])
+        tr = RemoteDMATransfer(dst_ids=[dest(c) for d, c in peers], dma_engine_mask=bits(lanes), remote_sem=T.sem["thr" + t],
+                               srcs=[T["mb" + t][:, 0:1]], dsts=[T["lt" + t][:, d:d + 1] for d, c in peers])
+        g.remote_dma_fused([tr], local_sem=T.sem.sent)
+        total["sent"] = total.get("sent", 0) + len(lanes)
+
+    for t in "01":
+        note("R", [v("land" + t, 16, 128), v("lands" + t, 16, 128)], [], ("arr" + t, 2 * arrive))
+        note("R", [v("lt" + t, 1, 8)], [], ("thr" + t, (N - 1) * len(lanes)))
+        total["arr" + t], total["thr" + t] = 2 * arrive, (N - 1) * len(lanes)
+
+    def bank(k):
+        return v("pm", 512 * k, 512 * k + 128)
+
+    def scores(t, jobs):
+        for k, b, m, col in jobs:
+            x = v("ex" + t, 128 * k, 128 * k + 128)
+            tt(x, bank(b), v(m), OP.mult)
+            total_s(v("sc" + t, col, col + 1), x, v("pen" + t, col, col + 1) if t == "1" else None)
+
+    def halves(t, k, part):
+        for b in range(4):
+            o, e, es = v("pn", 512 * b, 512 * b + 128), v("eq", 128 * b, 128 * b + 128), v("es", 128 * b, 128 * b + 128)
+            if part == 0:
+                mm(o, e, es, v("w" + t, 0, 128), v("ws" + t, 0, 128), True, False)
+            elif k < 2:
+                mm(o, e, es, v("g" + t, 128 * k, 128 * k + 128), v("gs" + t, 128 * k, 128 * k + 128), False, True)
+            else:
+                mm(o, e, es, v("land" + t), v("lands" + t), False, True)
+
+    def drain(t, k):
+        for b in range(4):
+            cp(v("nt" + t, 512 * k + b, 512 * k + 512, 4), v("pn", 512 * b, 512 * b + 128), "S")
+
+    def requant(t, k):
+        quant(v("w" + t, 128 * k + 128, 128 * k + 256), v("ws" + t, 128 * k + 128, 128 * k + 256), v("nt" + t, 512 * k, 512 * k + 512))
+
+    for t in "01":
+        W, WS, G, GS, L, LS, sc = "w" + t, "ws" + t, "g" + t, "gs" + t, "land" + t, "lands" + t, "sc" + t
+
+        def s_(a, b=None):
+            return v(sc, a, a + 1 if b is None else b)
+
+        send(t, 0)
+        send(t, 1)
+        mm(bank(0), v(W, 0, 128), v(WS, 0, 128), v(W, 0, 128), v(WS, 0, 128))
+        if t == "0":
+            for k in range(3):
+                ts(v("tli", 8 * k, 8 * k + 8), wp, 3, OP.mult, k, OP.add)
+            ts(v("tla"), v("tli"), 15, OP.bitwise_and)
+            ts(v("tlb"), v("tli"), 4, OP.arith_shift_right)
+            ts(fc(13), fc(12), 128 * r, OP.add)
+            ts(v("tlc"), v("tla"), 24, OP.mult)
+            tt(v("tla"), v("tlc"), v("tlb"), OP.add)
+            cp(v("tl"), v("tla"))
+            gather(v("prw", 128, 512), v("nbb"), v("tl"))
+            for k in range(2):
+                ts(v("e%d" % k), v("prw", 128 * k + 128, 128 * k + 256), fc(13), OP.is_equal)
+        scores(t, [(0, 0, "e0", 0), (1, 0, "e1", 1)])
+        best = v("mb" + t, 0, 1)
+        fill(v("mb" + t, 1, 32), 0.0)
+        fill(v("my" + t), 0.0)
+        fill(v("tq" + t, 0, 1), 0.0)
+        if t == "0":
+            for k in range(2):
+                tt(v("lm", 128 * k, 128 * k + 128), v("e%d" % k), v("ir"), OP.mult)
+        tt(best, s_(0), s_(1), OP.max)
+        send_best(t)
+        if t == "0":
+            for k in range(2):
+                total_s(fc(14 + k), v("lm", 128 * k, 128 * k + 128))
+            ts(fc(16), fc(15), 128, OP.mult, fc(14), OP.add)
+            wl = wrap("l", fc(16))
+            cp(v("lpi"), wl)
+            ts(v("lpa"), v("lpi"), 127, OP.bitwise_and)
+            ts(v("lpb"), v("lpi"), 7, OP.arith_shift_right)
+            cp(v("ll", 0, 8), v("lpa"))
+            cp(v("ll", 8, 16), v("lpb"))
+        pick(G, GS, 0, 256, W, WS, 0, 128, v("ll"))
+        if t == "0":
+            ts(v("eye"), v("npf"), 0, OP.is_equal)
+            fill(v("et"), 0.0)
+            ts(v("et", 4, 516, 4), v("eye"), 0.5, OP.mult)
+            for b in range(4):
+                quant(v("eq", 128 * b, 128 * b + 128), v("es", 128 * b, 128 * b + 128), v("et", 4 - b, 516 - b))
+            ts(ic(10), ic(0), 15, OP.bitwise_and)
+            ts(ic(11), ic(0), 1, OP.bitwise_and)
+            ts(ic(12), ic(0), 4, OP.arith_shift_right)
+            ts(fc(17), ic(11), -2, OP.mult, 1, OP.add)
+            cp(fc(18), ic(12))
+            tt(ic(13), ic(10), fc(17), OP.add)
+            ts(v("dm"), v("d8"), fc(18), OP.is_equal)
+            cp(v("swl", 0, 1), ic(13))
+            for k in range(3):
+                fill(v("wts", k, k + 1), 128.0 * (k + 1))
+            fill(v("wts", 3, 4), 1.0)
+        mm(bank(1), v(G, 0, 128), v(GS, 0, 128), v(G, 128, 256), v(GS, 128, 256))
+        mm(bank(2), v(G, 128, 256), v(GS, 128, 256), v(G, 0, 128), v(GS, 0, 128))
+        pick(L, LS, 0, 16, W, WS, 0, 128, v("swl", 0, 1))
+        halves(t, 0, 0)
+        halves(t, 0, 1)
+        if t == "1":
+            gather(v("selr"), v("ks"), v("vl0"), "S")
+            for k in range(2):
+                tt(v("selm", 128 * k, 128 * k + 128), v("selr"), v("e%d" % k), OP.mult)
+                total_s(fc(20 + k), v("selm", 128 * k, 128 * k + 128))
+            for col, who, k in ((2, 20, 2), (5, 20, 3), (3, 21, 1), (6, 21, 3)):
+                ts(v("pen1", col, col + 1), fc(who), k, OP.is_equal, -BIG / 128, OP.mult)
+        scores(t, [(2, 1, "e0", 2), (3, 2, "e1", 3)])
+        drain(t, 0)
+        halves(t, 1, 0)
+        halves(t, 1, 1)
+        turn(v("mx" + t, 0, 32, 1, 0, 32), v("mb" + t, 0, 32, 1, 0, 32))
+        cp(v("my" + t, 0, 16, 2, 0, 32), v("mx" + t, 1, 16, 2, 0, 32))
+        cp(v("my" + t, 1, 16, 2, 0, 32), v("mx" + t, 0, 16, 2, 0, 32))
+        turn(v("mz" + t, 0, 32, 1, 0, 32), v("my" + t, 0, 32, 1, 0, 32))
+        cp(v("tq" + t, 0, 1, 1, 0, 32), v("mz" + t, 0, 1, 1, 0, 32))
+        tt(s_(8), s_(1), s_(2), OP.max)
+        tt(s_(9), s_(0), s_(3), OP.max)
+        tt(s_(10), s_(8), s_(0), OP.is_gt)
+        tt(s_(11), s_(9), s_(1), OP.is_ge)
+        ts(s_(12), s_(10), -9 * BIG, OP.mult, s_(0), OP.add)
+        ts(s_(13), s_(11), -9 * BIG, OP.mult, s_(1), OP.add)
+        cp(v("met" + t, 3, 4), fc(3))
+        requant(t, 0)
+        drain(t, 1)
+        requant(t, 1)
+        halves(t, 2, 0)
+        if t == "1":
+            out, off, src = v("posr"), v("pl"), v("ir")
+            run("V", [out], [off, src], lambda: g.vector.tensor_copy(out[0].indirect(off[0]), src[0]))
+            tt(v("posm"), v("posr"), v("wm"), OP.mult)
+            scan(v("poss"), v("posm"))
+            cp(v("pol"), v("poss", 15, 128, 16))
+            fill(v("prw", 0, 128), -1.0)
+            gather(v("prs0"), v("prw"), v("vl0"), "S")
+            gather(v("pro0"), v("prs0"), v("pol"), "S")
+            dma("Y", "d_p0", T.pr[0:1, :], v("pro0", 0, 128, 1, 0, 1))
+            quant(v("wq"), v("wqs"), v("wt"))
+        mm(bank(0), v(W, 0, 128), v(WS, 0, 128), v(L), v(LS))
+        mm(bank(1), v(G, 0, 128), v(GS, 0, 128), v(L), v(LS))
+        mm(bank(2), v(G, 128, 256), v(GS, 128, 256), v(L), v(LS))
+        halves(t, 2, 1)
+        scores(t, [(4, 0, "eye", 4), (5, 1, "e0", 5), (6, 2, "e1", 6)])
+        drain(t, 2)
+        tt(v("tq" + t, 1, 8), v("lt" + t, 1, 8), v("dm", 1, 8), OP.mult)
+        red(s_(14), v("tq" + t), OP.add)
+        tt(s_(15), s_(14), best, OP.max)
+        tt(v("met" + t, 2, 3), s_(4), s_(15), OP.is_gt)
+        ts(s_(16, 18), s_(5, 7), s_(4), OP.max)
+        tt(v("met" + t, 0, 2), s_(12, 14), s_(16, 18), OP.is_ge)
+        tt(v("mew" + t), v("met" + t), v("wts"), OP.mult)
+        red(s_(18), v("mew" + t), OP.add)
+        wv = wrap("v" + t, s_(18))
+        cp(v("vl" + t), wv)
+        requant(t, 2)
+        if t == "0":
+            pick("w1", "ws1", 0, 128, W, WS, 0, 512, v("vl0"))
+            for k, col in ((0, 0), (1, 1), (2, 4)):
+                ts(v("pen1", col, col + 1), v("met0", k, k + 1), -BIG / 128, OP.mult)
+
+    pick("f0", "f0s", 0, 128, "w1", "ws1", 0, 512, v("vl1"))
+    pick("f1", "f1s", 0, 128, "f0", "f0s", 0, 128, v("pol"))
+    mm(bank(3), v("wq"), v("wqs"), v("f1"), v("f1s"))
+    f1 = v("f1")
+    dma("Y", "d_oc", T.oc[:, :], (T.f1[:, :].bitcast(dt.uint8),) + f1[1:])
+    gather(v("prs1"), v("prw"), v("vl1"), "S")
+    gather(v("pro1"), v("prs1"), v("pol"), "S")
+    cp(v("yo"), bank(3))
+    for k in range(4):
+        dma("Y" if k < 2 else "S", "d_os%d" % k, T.osc[4 * k:4 * k + 4, :], v("f1s", 0, 128, 1, 32 * k, 32 * k + 4))
+    dma("Y", "d_y", T.y[:, :], v("yo"))
+    dma("S", "d_p1", T.pr[1:2, :], v("pro1", 0, 128, 1, 0, 1))
+    for sem, n in total.items():
+        if waited.get(sem, 0) < n:
+            (g if sem == "sent" else g.sync).wait_ge(T.sem[sem], n)

@@ -2,48 +2,47 @@ from concourse.bass import DstId, RemoteDMATransfer
 from concourse.mybir import dt, AluOpType as OP, AxisListType, ActivationFunctionType as AF
 
 F32, BF16, I32, U16, U8, C4 = "float32", "bfloat16", "int32", "uint16", "uint8", "float8_e4m3fn_x4"
+SCRATCH = {"pn": ("psum", [128, 2048], F32), "pm": ("psum", [128, 2048], F32)}
 
-SCRATCH = {
-    "nbt": ("sbuf", [128, 3], I32), "nbr": ("sbuf", [128, 384], I32), "nbb": ("sbuf", [128, 384], I32),
-    "xt": ("sbuf", [128, 512], BF16), "wt": ("sbuf", [128, 512], BF16),
-    "icol": ("sbuf", [128, 32], I32), "fcol": ("sbuf", [128, 64], F32),
-    "cc3": ("sbuf", [128, 4], F32), "d8": ("sbuf", [128, 8], F32), "mk2": ("sbuf", [128, 4], F32), "dm": ("sbuf", [128, 8], F32),
-    "wts": ("sbuf", [128, 4], F32),
-    "npi": ("sbuf", [128, 128], I32), "npa": ("sbuf", [128, 128], I32), "npf": ("sbuf", [128, 128], F32), "ir": ("sbuf", [128, 128], F32),
-    "ones": ("sbuf", [128, 128], F32), "k128": ("sbuf", [128, 128], F32), "wm": ("sbuf", [128, 128], F32), "sm": ("sbuf", [128, 128], F32),
-    "eye": ("sbuf", [128, 128], F32), "ks": ("sbuf", [128, 512], F32),
-    "et": ("sbuf", [128, 520], BF16), "eq": ("sbuf", [128, 512], C4), "es": ("sbuf", [128, 512], U8),
-    "swl": ("sbuf", [128, 2], U16),
-    "n2m": ("sbuf", [128, 4], I32),
-    "zk": ("sbuf", [128, 128], F32), "rk": ("sbuf", [128, 128], F32), "sgn": ("sbuf", [128, 128], BF16),
-    "zx": ("sbuf", [128, 128], F32), "rx": ("sbuf", [128, 128], F32), "dx": ("sbuf", [128, 128], F32),
-    "pl": ("sbuf", [128, 8], U16), "tli": ("sbuf", [128, 24], I32), "tla": ("sbuf", [128, 24], I32), "tlb": ("sbuf", [128, 24], I32),
-    "tlc": ("sbuf", [128, 24], I32), "tl": ("sbuf", [128, 24], U16),
-    "prw": ("sbuf", [128, 512], F32), "e0": ("sbuf", [128, 128], BF16), "e1": ("sbuf", [128, 128], BF16),
-    "lm": ("sbuf", [128, 256], F32), "lpi": ("sbuf", [128, 8], I32), "lpa": ("sbuf", [128, 8], I32), "lpb": ("sbuf", [128, 8], I32), "ll": ("sbuf", [128, 16], U16),
-    "posr": ("sbuf", [128, 128], F32), "posm": ("sbuf", [128, 128], F32), "poss": ("sbuf", [128, 128], F32), "pol": ("sbuf", [128, 8], U16),
-    "selr": ("sbuf", [128, 128], F32), "selm": ("sbuf", [128, 256], F32),
-    "q0": ("sbuf", [128, 128], C4), "q0s": ("sbuf", [128, 128], U8),
-    "wq": ("sbuf", [128, 128], C4), "wqs": ("sbuf", [128, 128], U8),
-    "f0": ("sbuf", [128, 128], C4), "f0s": ("sbuf", [128, 128], U8), "f1": ("sbuf", [128, 128], C4), "f1s": ("sbuf", [128, 128], U8),
-    "yo": ("sbuf", [128, 128], F32),
-    "pn": ("psum", [128, 2048], F32), "pm": ("psum", [128, 2048], F32),
-}
-for _c in ("p", "l", "v0", "v1"):
-    SCRATCH["qz" + _c] = ("sbuf", [128, 128], F32)
-    SCRATCH["qt" + _c] = ("sbuf", [128, 128], F32)
-    SCRATCH["qs" + _c] = ("sbuf", [128, 128], F32)
+
+def _declare(dtype, width, names):
+    for n in names.split():
+        SCRATCH[n] = ("sbuf", [128, width], dtype)
+
+
+_declare(I32, 384, "nbr nbb")
+_declare(I32, 128, "npi npa")
+_declare(I32, 32, "icol")
+_declare(I32, 24, "tli tla tlb tlc")
+_declare(I32, 4, "nbt n2m")
+_declare(BF16, 520, "xt wt et")
+_declare(BF16, 128, "sgn e0 e1")
+_declare(F32, 64, "fcol")
+_declare(F32, 4, "cc3 mk2")
+_declare(F32, 8, "d8 dm")
+_declare(F32, 128, "npf npb n16 ir k128 wm sm eye zk rk zx rx dx posr posm poss selr yo xm0 xm1 xs0 xs1")
+_declare(F32, 256, "selm")
+_declare(F32, 512, "ks prw")
+_declare(U16, 24, "swl pl tl xl pol")
+_declare(C4, 512, "eq")
+_declare(U8, 512, "es")
+_declare(C4, 128, "q0 wq o1 f0 f1")
+_declare(U8, 128, "q0s wqs o1s f0s f1s")
+for _c in ("p", "v0", "v1"):
+    _declare(F32, 128, "qz%s qt%s qs%s" % (_c, _c, _c))
 for _t in "01":
-    SCRATCH.update({
-        "w" + _t: ("sbuf", [128, 512], C4), "ws" + _t: ("sbuf", [128, 512], U8),
-        "g" + _t: ("sbuf", [128, 256], C4), "gs" + _t: ("sbuf", [128, 256], U8),
-        "land" + _t: ("sbuf", [128, 128], C4), "lands" + _t: ("sbuf", [128, 128], U8),
-        "lt" + _t: ("sbuf", [128, 8], F32), "tq" + _t: ("sbuf", [128, 8], F32),
-        "mb" + _t: ("sbuf", [128, 32], F32), "mx" + _t: ("sbuf", [128, 32], F32), "my" + _t: ("sbuf", [128, 32], F32), "mz" + _t: ("sbuf", [128, 32], F32),
-        "sc" + _t: ("sbuf", [128, 32], F32), "pen" + _t: ("sbuf", [128, 8], F32), "met" + _t: ("sbuf", [128, 4], F32), "mew" + _t: ("sbuf", [128, 4], F32),
-        "ex" + _t: ("sbuf", [128, 1024], F32), "nt" + _t: ("sbuf", [128, 1536], BF16),
-        "vl" + _t: ("sbuf", [128, 8], U16), "prs" + _t: ("sbuf", [128, 128], F32), "pro" + _t: ("sbuf", [128, 128], F32),
-    })
+    _declare(C4, 512, "w" + _t)
+    _declare(U8, 512, "ws" + _t)
+    _declare(C4, 256, "g" + _t)
+    _declare(U8, 256, "gs" + _t)
+    _declare(C4, 128, "land" + _t)
+    _declare(U8, 128, "lands" + _t)
+    _declare(F32, 8, "lt%s tq%s pen%s met%s" % (_t, _t, _t, _t))
+    _declare(F32, 32, "mb%s mx%s my%s mz%s sc%s" % (_t, _t, _t, _t, _t))
+    _declare(F32, 1024, "ex" + _t)
+    _declare(BF16, 1536, "nt" + _t)
+    _declare(U16, 8, "vl" + _t)
+    _declare(F32, 128, "prs%s pro%s" % (_t, _t))
 DMAS = ["d_nbt", "d_nbr", "d_x", "d_w", "d_oc", "d_os0", "d_os1", "d_os2", "d_os3", "d_y", "d_p0", "d_p1"]
 SEMAPHORES = ["cV", "cS", "cT", "cG", "sent", "arr0", "arr1", "thr0", "thr1"] + DMAS
 BIG = 1e29
@@ -80,15 +79,18 @@ def rank_program(g, core, T, topo):
                 known[e][s] = max(known[e].get(s, 0), n)
 
     def order(e, outs, ins):
+        toks = {}
         for x in ins:
             psum = SCRATCH[x[1]][0] == "psum"
             for (y, tok, w, f) in hist.get(x[1], []):
                 if (w or (psum and f != e)) and meet(x, y):
-                    need(e, tok)
+                    toks[tok[0]] = max(toks.get(tok[0], 0), tok[1])
         for x in outs:
             for (y, tok, w, f) in hist.get(x[1], []):
                 if (f != e or e != "T") and meet(x, y):
-                    need(e, tok)
+                    toks[tok[0]] = max(toks.get(tok[0], 0), tok[1])
+        for s in sorted(toks, key=lambda s: s == "c" + e):
+            need(e, (s, toks[s]))
 
     def note(e, outs, ins, tok):
         for x in outs:
@@ -127,6 +129,12 @@ def rank_program(g, core, T, topo):
     def tt(out, a, b, op):
         run("V", [out], [a, b], lambda: g.vector.tensor_tensor(out[0], a[0], b[0], op))
 
+    def act(out, a, func, scale=1.0, bias=0.0, acc=None):
+        if acc is None:
+            run("S", [out], [a, bias], lambda: g.scalar.activation(out[0], a[0], func, bias=val(bias), scale=scale))
+        else:
+            run("S", [out, acc], [a, bias], lambda: g.scalar.activation(out[0], a[0], func, bias=val(bias), scale=scale, accum_out=acc[0]))
+
     def cp(out, a, e="V"):
         if e == "V":
             run("V", [out], [a], lambda: g.vector.tensor_copy(out[0], a[0]))
@@ -138,12 +146,6 @@ def rank_program(g, core, T, topo):
 
     def red(out, a, op, ab=False):
         run("V", [out], [a], lambda: g.vector.tensor_reduce(out[0], a[0], AxisListType.X, op, apply_absolute_value=ab))
-
-    def total_s(out, a, bias=None):
-        if bias is None:
-            run("S", [out, a], [a], lambda: g.scalar.activation(a[0], a[0], AF.Copy, accum_out=out[0]))
-        else:
-            run("S", [out, a], [a, bias], lambda: g.scalar.activation(a[0], a[0], AF.Identity, bias=bias[0], accum_out=out[0]))
 
     def turn(out, a):
         run("V", [out], [a], lambda: g.vector.transpose(out[0], a[0]))
@@ -167,21 +169,23 @@ def rank_program(g, core, T, topo):
         run("V", [o], [w, off], lambda: g.vector.tensor_copy(o[0].bitcast(dt.uint32), w[0].bitcast(dt.uint32).indirect(off[0])))
         gather(v(os, oa, ob), v(isc, ia, ib), off, "S")
 
-    def iota(out, pattern, base, cm, flag):
+    def iota(out, pattern, base, cm, flag=True):
         run("G", [out], [], lambda: g.iota(out[0], pattern, base, cm, allow_small_or_imprecise_dtypes=True) if flag else g.iota(out[0], pattern, base, cm))
 
-    def quarters(name, c0, st):
+    def quarters(name, c0, st, mid=None):
         for e, d in (("V", 0), ("S", 1), ("V", 2), ("S", 3)):
             a = d ^ 1
-            cp(v(name, 32 * a + c0, 32 * a + 32, st, 32 * d, 32 * d + 32), v(name, 32 * a + c0, 32 * a + 32, st, 32 * a, 32 * a + 32), e)
+            cp(v(name, 32 * a + c0, 32 * a + 32, st, 32 * d, 32 * d + 32), v(name, 32 * a + c0, 32 * a + 32, st, 32 * a, 32 * a + 32), "S" if mid else e)
+        if mid:
+            mid()
         cp(v(name, 64 + c0, 128, st, 0, 64), v(name, 64 + c0, 128, st, 64, 128), "V")
         cp(v(name, c0, 64, st, 64, 128), v(name, c0, 64, st, 0, 64), "S")
 
-    def wrap(tag, col):
+    def wrap(tag, col, mid):
         ts(v("qz" + tag), v("wm"), col, OP.mult)
         turn(v("qt" + tag), v("qz" + tag))
         scan(v("qs" + tag), v("qt" + tag))
-        quarters("qs" + tag, 15, 16)
+        quarters("qs" + tag, 15, 16, mid)
         return v("qs" + tag, 15, 128, 16)
 
     def ic(k):
@@ -190,17 +194,19 @@ def rank_program(g, core, T, topo):
     def fc(k):
         return v("fcol", k, k + 1)
 
-    dma("Y", "d_nbt", v("nbt"), T.nb[:, :])
-    dma("S", "d_x", v("xt"), T.x[:, :])
+    dma("Y", "d_nbt", v("nbt", 0, 3), T.nb[:, :])
+    dma("S", "d_x", v("xt", 0, 512), T.x[:, :])
     dma("Y", "d_nbr", v("nbr", 0, 384, 1, 0, 1), T.nb[:, :])
-    dma("Y", "d_w", v("wt"), T.w[:, :])
+    dma("Y", "d_w", v("wt", 0, 512), T.w[:, :])
 
     iota(ic(0), [[0, 1]], 0, 1, False)
-    iota(v("cc3", 0, 3), [[1, 3]], 0, 0, True)
+    iota(v("cc3", 0, 3), [[1, 3]], 0, 0)
     iota(v("npi"), [[1, 128]], 128, -1, False)
-    fill(v("ones"), 1.0)
-    fill(v("k128"), 128.0)
-    fill(v("sm"), 1.0)
+    iota(v("npf"), [[1, 128]], 0, -1)
+    iota(v("n16"), [[0, 8], [1, 16]], 0, 0)
+    iota(v("k128"), [[0, 128]], 128, 0)
+    iota(v("d8"), [[1, 8]], 0, 0)
+    fill(v("et"), 0.0)
     ts(ic(1), ic(0), 3, OP.arith_shift_right)
     ts(ic(2), ic(0), 7, OP.bitwise_and)
     ts(ic(6), ic(0), 16 * r, OP.bitwise_and)
@@ -218,47 +224,54 @@ def rank_program(g, core, T, topo):
     ts(fc(7), fc(5), 128 * 127, OP.add)
     ts(fc(8), fc(4), 16 * r, OP.add, 256, OP.mult)
     ts(v("npa"), v("npi"), 15, OP.bitwise_and)
-    fill(v("sm", 0, 128, 16), 0.0)
     ts(v("wm"), v("npa"), 0, OP.is_equal)
+    act(v("npb"), v("npf"), AF.Abs)
+    act(v("sm"), v("n16"), AF.Sign)
+    act(v("eye"), v("npb"), AF.Relu, -1.0, 1.0)
+    act(v("et", 4, 516, 4), v("eye"), AF.Copy, 0.5)
 
-    tt(v("n2m", 0, 3), v("nbt"), v("mk2", 0, 3), OP.mult)
+    tt(v("n2m", 0, 3), v("nbt", 0, 3), v("mk2", 0, 3), OP.mult)
     red(ic(8), v("n2m", 0, 3), OP.max)
     ts(ic(9), ic(8), 896, OP.bitwise_and)
     ts(fc(9), ic(8), 0.5, OP.add, fc(6), OP.min)
     ts(fc(10), ic(9), 8, OP.mult, fc(9), OP.add)
-    ts(v("zk"), v("ones"), fc(10), OP.mult)
+    ts(v("zk"), v("npf"), 0.0, OP.mult, fc(10), OP.add)
     turn(v("rk"), v("zk"))
     quarters("rk", 0, 1)
-    kk, kb, sg, ac = v("rk"), fc(10), v("sgn"), fc(11)
-    run("S", [sg, ac], [kk, kb], lambda: g.scalar.activation(sg[0], kk[0], AF.Sign, bias=kb[0], scale=-1.0, accum_out=ac[0]))
-    iota(v("ir"), [[1, 128]], 0, 0, True)
+    act(v("sgn"), v("rk"), AF.Sign, -1.0, fc(10), fc(11))
     nb1, nball = v("nbr", 0, 384, 1, 0, 1), v("nbb")
     run("G", [nball], [nb1], lambda: g.partition_broadcast(nball[0], nb1[0], 128))
-    iota(v("npf"), [[1, 128]], 0, -1, True)
-    iota(v("d8"), [[1, 8]], 0, 0, True)
-    iota(v("ks"), [[1, 4], [0, 128]], 0, 0, True)
+    iota(v("ir"), [[1, 128]], 0, 0)
+    iota(v("ks"), [[1, 4], [0, 128]], 0, 0)
+    for t in "01":
+        fill(v("mb" + t, 1, 32), 0.0)
+        fill(v("my" + t), 0.0)
+        fill(v("tq" + t, 0, 1), 0.0)
     ts(v("zx"), v("k128"), fc(11), OP.mult, fc(7), OP.add)
     turn(v("rx"), v("zx"))
     quarters("rx", 0, 1)
     ts(v("dx"), v("rx"), fc(8), OP.subtract)
     red(fc(12), v("dx"), OP.min, True)
-    wp = wrap("p", fc(12))
-    cp(v("pl"), wp)
-    quant(v("q0"), v("q0s"), v("xt"))
-    pick("w0", "ws0", 0, 128, "q0", "q0s", 0, 128, v("pl"))
+    wp = wrap("p", fc(12), lambda: quant(v("q0"), v("q0s"), v("xt", 0, 512)))
+    cp(v("pl", 0, 8), wp)
+    pick("w0", "ws0", 0, 128, "q0", "q0s", 0, 128, v("pl", 0, 8))
 
     peers = [(d, cores[r ^ d]) for d in range(1, N)]
     chip = topo.cores_of(core)
     far = [(d, c) for d, c in peers if c not in chip]
     near = [(d, c) for d, c in peers if c in chip]
     lanes = topo.engines(core, far[0][1])
-    ways = {}
-    for k, (d, c) in enumerate(far):
-        ways[d] = [lanes[k]]
-    rest = lanes[len(far):]
-    for k, (d, c) in enumerate(near):
-        ways[d] = rest[k::len(near)]
-    arrive = sum(len(x) for x in ways.values())
+    spare = 2 * len(far) - len(lanes)
+    ways = []
+    for part in range(2):
+        mine = lanes[spare:] + lanes[:spare] if part else lanes
+        way = {}
+        for k, (d, c) in enumerate(far):
+            way[d] = [mine[k]] if k < spare else [mine[spare + 2 * (k - spare)], mine[spare + 2 * (k - spare) + 1]]
+        for d, c in near:
+            way[d] = [e for e in topo.engines(core, c) if e not in lanes][:2]
+        ways.append(way)
+    arrive = sum(len(x) for w in ways for x in w.values())
 
     def bits(es):
         return sum(1 << e for e in es)
@@ -275,9 +288,9 @@ def rank_program(g, core, T, topo):
             a, b = T[name][:, 16 * d:16 * d + 16], T[dst][:, 16 * d:16 * d + 16]
             if part == 0:
                 a, b = a.bitcast(dt.uint8), b.bitcast(dt.uint8)
-            tr.append(RemoteDMATransfer(dst_ids=[dest(c)], dma_engine_mask=bits(ways[d]), remote_sem=T.sem["arr" + t], src=a, dst=b))
+            tr.append(RemoteDMATransfer(dst_ids=[dest(c)], dma_engine_mask=bits(ways[part][d]), remote_sem=T.sem["arr" + t], src=a, dst=b))
         g.remote_dma_fused(tr, local_sem=T.sem.sent)
-        total["sent"] = total.get("sent", 0) + arrive
+        total["sent"] = total.get("sent", 0) + sum(len(x) for x in ways[part].values())
 
     def send_best(t):
         order("G", [], [v("mb" + t, 0, 1)])
@@ -287,18 +300,21 @@ def rank_program(g, core, T, topo):
         total["sent"] = total.get("sent", 0) + len(lanes)
 
     for t in "01":
-        note("R", [v("land" + t, 16, 128), v("lands" + t, 16, 128)], [], ("arr" + t, 2 * arrive))
-        note("R", [v("lt" + t, 1, 8)], [], ("thr" + t, (N - 1) * len(lanes)))
-        total["arr" + t], total["thr" + t] = 2 * arrive, (N - 1) * len(lanes)
+        total["arr" + t], total["thr" + t] = arrive, (N - 1) * len(lanes)
+        note("R", [v("land" + t, 16, 128), v("lands" + t, 16, 128)], [], ("arr" + t, total["arr" + t]))
+        note("R", [v("lt" + t, 1, 8)], [], ("thr" + t, total["thr" + t]))
 
     def bank(k):
         return v("pm", 512 * k, 512 * k + 128)
 
     def scores(t, jobs):
         for k, b, m, col in jobs:
-            x = v("ex" + t, 128 * k, 128 * k + 128)
+            x, out = v("ex" + t, 128 * k, 128 * k + 128), v("sc" + t, col, col + 1)
             tt(x, bank(b), v(m), OP.mult)
-            total_s(v("sc" + t, col, col + 1), x, v("pen" + t, col, col + 1) if t == "1" else None)
+            if t == "0":
+                act(x, x, AF.Copy, acc=out)
+            else:
+                act(x, x, AF.Identity, bias=v("pen1", col, col + 1), acc=out)
 
     def halves(t, k, part):
         for b in range(4):
@@ -318,10 +334,13 @@ def rank_program(g, core, T, topo):
         quant(v("w" + t, 128 * k + 128, 128 * k + 256), v("ws" + t, 128 * k + 128, 128 * k + 256), v("nt" + t, 512 * k, 512 * k + 512))
 
     for t in "01":
-        W, WS, G, GS, L, LS, sc = "w" + t, "ws" + t, "g" + t, "gs" + t, "land" + t, "lands" + t, "sc" + t
+        W, WS, G, GS, L, LS, sc, met = "w" + t, "ws" + t, "g" + t, "gs" + t, "land" + t, "lands" + t, "sc" + t, "met" + t
 
         def s_(a, b=None):
             return v(sc, a, a + 1 if b is None else b)
+
+        def m_(a):
+            return v(met, a, a + 1)
 
         send(t, 0)
         send(t, 1)
@@ -335,34 +354,26 @@ def rank_program(g, core, T, topo):
             ts(v("tlc"), v("tla"), 24, OP.mult)
             tt(v("tla"), v("tlc"), v("tlb"), OP.add)
             cp(v("tl"), v("tla"))
-            gather(v("prw", 128, 512), v("nbb"), v("tl"))
+            gather(v("prw", 128, 384), v("nbb"), v("tl", 0, 16))
             for k in range(2):
                 ts(v("e%d" % k), v("prw", 128 * k + 128, 128 * k + 256), fc(13), OP.is_equal)
-        scores(t, [(0, 0, "e0", 0), (1, 0, "e1", 1)])
+        else:
+            pick("o1", "o1s", 0, 128, W, WS, 0, 128, v("pol", 0, 8))
+        scores(t, [(0, 0, "e0", 1), (1, 0, "e1", 0)])
         best = v("mb" + t, 0, 1)
-        fill(v("mb" + t, 1, 32), 0.0)
-        fill(v("my" + t), 0.0)
-        fill(v("tq" + t, 0, 1), 0.0)
         if t == "0":
-            for k in range(2):
-                tt(v("lm", 128 * k, 128 * k + 128), v("e%d" % k), v("ir"), OP.mult)
+            out, off, src = v("posr"), v("pl", 0, 8), v("ir")
+            run("V", [out], [off, src], lambda: g.vector.tensor_copy(out[0].indirect(off[0]), src[0]))
         tt(best, s_(0), s_(1), OP.max)
         send_best(t)
         if t == "0":
             for k in range(2):
-                total_s(fc(14 + k), v("lm", 128 * k, 128 * k + 128))
-            ts(fc(16), fc(15), 128, OP.mult, fc(14), OP.add)
-            wl = wrap("l", fc(16))
-            cp(v("lpi"), wl)
-            ts(v("lpa"), v("lpi"), 127, OP.bitwise_and)
-            ts(v("lpb"), v("lpi"), 7, OP.arith_shift_right)
-            cp(v("ll", 0, 8), v("lpa"))
-            cp(v("ll", 8, 16), v("lpb"))
-        pick(G, GS, 0, 256, W, WS, 0, 128, v("ll"))
-        if t == "0":
-            ts(v("eye"), v("npf"), 0, OP.is_equal)
-            fill(v("et"), 0.0)
-            ts(v("et", 4, 516, 4), v("eye"), 0.5, OP.mult)
+                tt(v("xm%d" % k), v("prw", 128 * k + 128, 128 * k + 256), v("wm"), OP.mult)
+            for k in range(2):
+                scan(v("xs%d" % k), v("xm%d" % k))
+            for k in range(2):
+                ts(v("xl", 8 * k, 8 * k + 8), v("xs%d" % k, 15, 128, 16), -128 * r, OP.add)
+            pick(G, GS, 0, 256, "q0", "q0s", 0, 128, v("xl", 0, 16))
             for b in range(4):
                 quant(v("eq", 128 * b, 128 * b + 128), v("es", 128 * b, 128 * b + 128), v("et", 4 - b, 516 - b))
             ts(ic(10), ic(0), 15, OP.bitwise_and)
@@ -370,12 +381,10 @@ def rank_program(g, core, T, topo):
             ts(ic(12), ic(0), 4, OP.arith_shift_right)
             ts(fc(17), ic(11), -2, OP.mult, 1, OP.add)
             cp(fc(18), ic(12))
-            tt(ic(13), ic(10), fc(17), OP.add)
+            ts(v("swl", 0, 1), ic(10), fc(17), OP.add)
             ts(v("dm"), v("d8"), fc(18), OP.is_equal)
-            cp(v("swl", 0, 1), ic(13))
-            for k in range(3):
-                fill(v("wts", k, k + 1), 128.0 * (k + 1))
-            fill(v("wts", 3, 4), 1.0)
+        else:
+            pick(G, GS, 0, 256, "o1", "o1s", 0, 128, v("xl", 0, 16))
         mm(bank(1), v(G, 0, 128), v(GS, 0, 128), v(G, 128, 256), v(GS, 128, 256))
         mm(bank(2), v(G, 128, 256), v(GS, 128, 256), v(G, 0, 128), v(GS, 0, 128))
         pick(L, LS, 0, 16, W, WS, 0, 128, v("swl", 0, 1))
@@ -384,9 +393,10 @@ def rank_program(g, core, T, topo):
         if t == "1":
             gather(v("selr"), v("ks"), v("vl0"), "S")
             for k in range(2):
-                tt(v("selm", 128 * k, 128 * k + 128), v("selr"), v("e%d" % k), OP.mult)
-                total_s(fc(20 + k), v("selm", 128 * k, 128 * k + 128))
-            for col, who, k in ((2, 20, 2), (5, 20, 3), (3, 21, 1), (6, 21, 3)):
+                x = v("selm", 128 * k, 128 * k + 128)
+                tt(x, v("selr"), v("e%d" % k), OP.mult)
+                act(x, x, AF.Copy, acc=fc(20 + k))
+            for col, who, k in ((2, 20, 2), (3, 21, 1), (5, 20, 3), (6, 21, 3)):
                 ts(v("pen1", col, col + 1), fc(who), k, OP.is_equal, -BIG / 128, OP.mult)
         scores(t, [(2, 1, "e0", 2), (3, 2, "e1", 3)])
         drain(t, 0)
@@ -397,28 +407,26 @@ def rank_program(g, core, T, topo):
         cp(v("my" + t, 1, 16, 2, 0, 32), v("mx" + t, 0, 16, 2, 0, 32))
         turn(v("mz" + t, 0, 32, 1, 0, 32), v("my" + t, 0, 32, 1, 0, 32))
         cp(v("tq" + t, 0, 1, 1, 0, 32), v("mz" + t, 0, 1, 1, 0, 32))
-        tt(s_(8), s_(1), s_(2), OP.max)
-        tt(s_(9), s_(0), s_(3), OP.max)
-        tt(s_(10), s_(8), s_(0), OP.is_gt)
-        tt(s_(11), s_(9), s_(1), OP.is_ge)
-        ts(s_(12), s_(10), -9 * BIG, OP.mult, s_(0), OP.add)
-        ts(s_(13), s_(11), -9 * BIG, OP.mult, s_(1), OP.add)
-        cp(v("met" + t, 3, 4), fc(3))
+        tt(s_(8, 10), s_(0, 2), s_(2, 4), OP.max)
+        ts(s_(10), s_(8), s_(1), OP.is_gt, -9 * BIG, OP.mult)
+        ts(s_(11), s_(9), s_(0), OP.is_ge, -9 * BIG, OP.mult)
+        tt(s_(12), s_(10), s_(1), OP.add)
+        tt(s_(13), s_(11), s_(0), OP.add)
         requant(t, 0)
         drain(t, 1)
         requant(t, 1)
         halves(t, 2, 0)
-        if t == "1":
-            out, off, src = v("posr"), v("pl"), v("ir")
-            run("V", [out], [off, src], lambda: g.vector.tensor_copy(out[0].indirect(off[0]), src[0]))
+        if t == "0":
             tt(v("posm"), v("posr"), v("wm"), OP.mult)
             scan(v("poss"), v("posm"))
-            cp(v("pol"), v("poss", 15, 128, 16))
+            cp(v("pol", 0, 8), v("poss", 15, 128, 16))
+        else:
             fill(v("prw", 0, 128), -1.0)
+            gather(v("prw", 384, 512), v("nbb"), v("tl", 16, 24))
             gather(v("prs0"), v("prw"), v("vl0"), "S")
-            gather(v("pro0"), v("prs0"), v("pol"), "S")
+            gather(v("pro0"), v("prs0"), v("pol", 0, 8), "S")
             dma("Y", "d_p0", T.pr[0:1, :], v("pro0", 0, 128, 1, 0, 1))
-            quant(v("wq"), v("wqs"), v("wt"))
+            quant(v("wq"), v("wqs"), v("wt", 0, 512))
         mm(bank(0), v(W, 0, 128), v(WS, 0, 128), v(L), v(LS))
         mm(bank(1), v(G, 0, 128), v(GS, 0, 128), v(L), v(LS))
         mm(bank(2), v(G, 128, 256), v(GS, 128, 256), v(L), v(LS))
@@ -427,27 +435,26 @@ def rank_program(g, core, T, topo):
         drain(t, 2)
         tt(v("tq" + t, 1, 8), v("lt" + t, 1, 8), v("dm", 1, 8), OP.mult)
         red(s_(14), v("tq" + t), OP.add)
-        tt(s_(15), s_(14), best, OP.max)
-        tt(v("met" + t, 2, 3), s_(4), s_(15), OP.is_gt)
-        ts(s_(16, 18), s_(5, 7), s_(4), OP.max)
-        tt(v("met" + t, 0, 2), s_(12, 14), s_(16, 18), OP.is_ge)
-        tt(v("mew" + t), v("met" + t), v("wts"), OP.mult)
-        red(s_(18), v("mew" + t), OP.add)
-        wv = wrap("v" + t, s_(18))
+        ts(m_(2), s_(14), best, OP.max, s_(4), OP.is_lt)
+        ts(m_(0), s_(5), s_(4), OP.max, s_(12), OP.is_le)
+        ts(s_(15), m_(2), 384, OP.mult, fc(3), OP.add)
+        ts(m_(1), s_(6), s_(4), OP.max, s_(13), OP.is_le)
+        ts(s_(16), m_(0), 128, OP.mult, s_(15), OP.add)
+        ts(s_(18), m_(1), 256, OP.mult, s_(16), OP.add)
+        wv = wrap("v" + t, s_(18), lambda: requant(t, 2))
         cp(v("vl" + t), wv)
-        requant(t, 2)
         if t == "0":
             pick("w1", "ws1", 0, 128, W, WS, 0, 512, v("vl0"))
-            for k, col in ((0, 0), (1, 1), (2, 4)):
-                ts(v("pen1", col, col + 1), v("met0", k, k + 1), -BIG / 128, OP.mult)
+            for k, col in ((1, 0), (0, 1), (2, 4)):
+                ts(v("pen1", col, col + 1), m_(k), -BIG / 128, OP.mult)
 
     pick("f0", "f0s", 0, 128, "w1", "ws1", 0, 512, v("vl1"))
-    pick("f1", "f1s", 0, 128, "f0", "f0s", 0, 128, v("pol"))
+    pick("f1", "f1s", 0, 128, "f0", "f0s", 0, 128, v("pol", 0, 8))
     mm(bank(3), v("wq"), v("wqs"), v("f1"), v("f1s"))
     f1 = v("f1")
     dma("Y", "d_oc", T.oc[:, :], (T.f1[:, :].bitcast(dt.uint8),) + f1[1:])
     gather(v("prs1"), v("prw"), v("vl1"), "S")
-    gather(v("pro1"), v("prs1"), v("pol"), "S")
+    gather(v("pro1"), v("prs1"), v("pol", 0, 8), "S")
     cp(v("yo"), bank(3))
     for k in range(4):
         dma("Y" if k < 2 else "S", "d_os%d" % k, T.osc[4 * k:4 * k + 4, :], v("f1s", 0, 128, 1, 32 * k, 32 * k + 4))

@@ -10,24 +10,24 @@ def _declare(dtype, width, names):
         SCRATCH[n] = ("sbuf", [128, width], dtype)
 
 
-_declare(I32, 384, "nbr nbb")
-_declare(I32, 128, "npi npa")
-_declare(I32, 32, "icol")
-_declare(I32, 24, "tli tla tlb tlc")
-_declare(I32, 4, "nbt n2m")
+_declare(I32, 72, "nl")
+_declare(I32, 16, "icol")
+_declare(I32, 8, "nbt")
 _declare(BF16, 520, "xt wt et")
-_declare(BF16, 128, "sgn e0 e1")
+_declare(BF16, 128, "sgn")
 _declare(F32, 64, "fcol")
-_declare(F32, 4, "cc3 mk2")
-_declare(F32, 8, "d8 dm")
-_declare(F32, 128, "npf npb n16 ir k128 wm sm eye zk rk zx rx dx posr posm poss selr yo xm0 xm1 xs0 xs1")
-_declare(F32, 256, "selm")
-_declare(F32, 512, "ks prw")
-_declare(U16, 24, "swl pl tl xl pol")
+_declare(F32, 24, "d24")
+_declare(F32, 32, "lf lft")
+_declare(F32, 8, "dmb")
+_declare(F32, 128, "mq npf npb n16 k128 wm sm eye zk rk zx rx dx e0 e1 posn posm poss yo xm0 xm1 xs0 xs1")
+_declare(F32, 256, "selm npos nsl")
+_declare(F32, 384, "nbp")
+_declare(F32, 512, "ks pa")
+_declare(U16, 24, "nlu pl swl cl xsl pol")
 _declare(C4, 512, "eq")
 _declare(U8, 512, "es")
-_declare(C4, 128, "q0 wq o1 f0 f1")
-_declare(U8, 128, "q0s wqs o1s f0s f1s")
+_declare(C4, 128, "q0 wq f0 f1")
+_declare(U8, 128, "q0s wqs f0s f1s")
 for _c in ("p", "v0", "v1"):
     _declare(F32, 128, "qz%s qt%s qs%s" % (_c, _c, _c))
 for _t in "01":
@@ -37,15 +37,18 @@ for _t in "01":
     _declare(U8, 256, "gs" + _t)
     _declare(C4, 128, "land" + _t)
     _declare(U8, 128, "lands" + _t)
-    _declare(F32, 8, "lt%s tq%s pen%s met%s" % (_t, _t, _t, _t))
-    _declare(F32, 32, "mb%s mx%s my%s mz%s sc%s" % (_t, _t, _t, _t, _t))
+    _declare(F32, 8, "lt%s cq%s s4m%s pen%s met%s" % (_t, _t, _t, _t, _t))
+    _declare(F32, 32, "mx%s sc%s" % (_t, _t))
     _declare(F32, 1024, "ex" + _t)
     _declare(BF16, 1536, "nt" + _t)
     _declare(U16, 8, "vl" + _t)
     _declare(F32, 128, "prs%s pro%s" % (_t, _t))
-DMAS = ["d_nbt", "d_nbr", "d_x", "d_w", "d_oc", "d_os0", "d_os1", "d_os2", "d_os3", "d_y", "d_p0", "d_p1"]
+DMAS = ["d_nbt", "d_n0", "d_n1", "d_n2", "d_x", "d_w", "d_nbp", "d_oc", "d_os0", "d_os1", "d_os2", "d_os3", "d_y", "d_p0", "d_p1"]
 SEMAPHORES = ["cV", "cS", "cT", "cG", "sent", "arr0", "arr1", "thr0", "thr1"] + DMAS
 BIG = 1e29
+WAKE, TENS, LOAD, ISSUE, FLIGHT = 100.0, 110.0, 1500.0, 600.0, 4500.0
+LOOK = 250.0
+WHOLE = 12582912.0
 
 
 def rank_program(g, core, T, topo):
@@ -62,8 +65,8 @@ def rank_program(g, core, T, topo):
         c1 = SCRATCH[name][1][1] if c1 is None else c1
         ap = T[name][p0:p1, c0:c1] if st == 1 else T[name][p0:p1, c0:c1:st]
         if SCRATCH[name][0] == "psum":
-            return (ap, name, 0, 128, c0 // 512 * 512, (c1 + 511) // 512 * 512, 1)
-        return (ap, name, p0, p1, c0, c1, st)
+            return (ap, name, 0, 128, c0 // 512 * 512, (c1 + 511) // 512 * 512, 1, 128)
+        return (ap, name, p0, p1, c0, c1, st, (c1 - c0 + st - 1) // st)
 
     def meet(a, b):
         if a[3] <= b[2] or b[3] <= a[2] or a[5] <= b[4] or b[5] <= a[4]:
@@ -98,94 +101,181 @@ def rank_program(g, core, T, topo):
         for x in ins:
             hist.setdefault(x[1], []).append((x, tok, False, e))
 
-    def run(e, outs, ins, call):
-        outs = [x for x in outs if isinstance(x, tuple)]
-        ins = [x for x in ins if isinstance(x, tuple)]
-        order(e, outs, ins)
-        count[e] += 1
-        tok = ("c" + e, count[e])
-        call().then_inc(T.sem[tok[0]], 1)
-        total[tok[0]] = count[e]
-        snap[tok] = dict(known[e])
-        note(e, outs, ins, tok)
+    ops, seen = [], {}
+
+    def views(xs):
+        return [x for x in xs if isinstance(x, tuple)]
+
+    def add(outs, ins, emit, cost, late=0.0, after=()):
+        e, outs, ins = "".join(cost), views(outs), views(ins)
+        i, deps = len(ops), set(after)
+        for x in ins:
+            psum = SCRATCH[x[1]][0] == "psum"
+            deps.update(j for y, j, w, f in seen.get(x[1], []) if (w or (psum and f != e)) and meet(x, y))
+        for x in outs:
+            deps.update(j for y, j, w, f in seen.get(x[1], []) if meet(x, y))
+        for x in outs:
+            seen.setdefault(x[1], []).append((x, i, True, e))
+        for x in ins:
+            seen.setdefault(x[1], []).append((x, i, False, e))
+        ops.append((emit, cost, late, sorted(deps)))
+        return i
+
+    def run(outs, ins, call, cost):
+        outs, ins = views(outs), views(ins)
+
+        def emit(e):
+            order(e, outs, ins)
+            count[e] += 1
+            tok = ("c" + e, count[e])
+            call(e).then_inc(T.sem[tok[0]], 1)
+            total[tok[0]] = count[e]
+            snap[tok] = dict(known[e])
+            note(e, outs, ins, tok)
+        add(outs, ins, emit, cost)
+
+    def schedule():
+        n = len(ops)
+        users = [[] for _ in ops]
+        for i, o in enumerate(ops):
+            for j in o[3]:
+                users[j].append(i)
+        way = [0.0] * n
+        for i in range(n - 1, -1, -1):
+            way[i] = min(ops[i][1].values()) + ops[i][2] + max([way[j] + WAKE for j in users[i]] + [0.0])
+        left, end, free = [len(o[3]) for o in ops], [0.0] * n, {}
+        ready = {i: 0.0 for i in range(n) if not left[i]}
+        when = []
+        while ready:
+            best = None
+            for e in "RVSTGY":
+                c = [(s, i) for i, s in ready.items() if e in ops[i][1]]
+                if not c:
+                    continue
+                t = free.get(e, 0.0)
+                if e == "R":
+                    x, t = min(c), 0.0
+                elif e == "G":
+                    x = min(c, key=lambda y: y[1])
+                else:
+                    t0 = max(t, min(c)[0])
+                    x = max([y for y in c if y[0] <= t0 + LOOK], key=lambda y: (way[y[1]] - max(0.0, y[0] - t0), -y[1]))
+                    if x[0] > t0:
+                        fit = [y for y in c if max(t, y[0]) + ops[y[1]][1][e] <= x[0]]
+                        if fit:
+                            x = max(fit, key=lambda y: (way[y[1]], -y[1]))
+                s = max(t, x[0])
+                z = s + ops[x[1]][1][e]
+                if best is None or (s, z) < best[:2]:
+                    best = (s, z, e, x[1])
+            s, z, e, i = best
+            end[i] = z + ops[i][2]
+            free[e] = z
+            when.append((s, len(when), e, i))
+            del ready[i]
+            for j in users[i]:
+                left[j] -= 1
+                if not left[j]:
+                    ready[j] = max(end[m] for m in ops[j][3]) + WAKE
+        for s, k, e, i in when:
+            if e != "R":
+                ops[i][0](e)
 
     def val(x):
         return x[0] if isinstance(x, tuple) else x
 
-    def dma(e, sem, out, in_):
-        outs, ins = [x for x in (out,) if isinstance(x, tuple)], [x for x in (in_,) if isinstance(x, tuple)]
-        order(e, outs, ins)
-        queue[e].dma_start(val(out), val(in_)).then_inc(T.sem[sem], 16)
-        total[sem] = 16
-        snap[(sem, 16)] = dict(known[e])
-        note("D" + sem, outs, ins, (sem, 16))
+    def dma(e, sem, *moves):
+        outs, ins = views([x for x, y in moves]), views([y for x, y in moves])
+
+        def emit(e):
+            for out, in_ in moves:
+                order(e, views([out]), views([in_]))
+                queue[e].dma_start(val(out), val(in_)).then_inc(T.sem[sem], 16)
+            total[sem] = 16 * len(moves)
+            snap[(sem, total[sem])] = dict(known[e])
+            note("D" + sem, outs, ins, (sem, total[sem]))
+        add(outs, ins, emit, {e: 60.0 * len(moves)}, LOAD)
+
+    def vec(x, a=1.0):
+        return max(64, a * x[7]) * 0.83
 
     def ts(out, a, s1, op0, s2=None, op1=None):
         if op1 is None:
-            run("V", [out], [a, s1], lambda: g.vector.tensor_scalar(out[0], a[0], val(s1), None, op0))
+            run([out], [a, s1], lambda e: g.vector.tensor_scalar(out[0], a[0], val(s1), None, op0), {"V": vec(a)})
         else:
-            run("V", [out], [a, s1, s2], lambda: g.vector.tensor_scalar(out[0], a[0], val(s1), val(s2), op0, op1))
+            run([out], [a, s1, s2], lambda e: g.vector.tensor_scalar(out[0], a[0], val(s1), val(s2), op0, op1), {"V": vec(a)})
 
     def tt(out, a, b, op):
-        run("V", [out], [a, b], lambda: g.vector.tensor_tensor(out[0], a[0], b[0], op))
+        run([out], [a, b], lambda e: g.vector.tensor_tensor(out[0], a[0], b[0], op), {"V": vec(a, 1 if a[1] in ("pn", "pm") else 2)})
 
     def act(out, a, func, scale=1.0, bias=0.0, acc=None):
         if acc is None:
-            run("S", [out], [a, bias], lambda: g.scalar.activation(out[0], a[0], func, bias=val(bias), scale=scale))
+            run([out], [a, bias], lambda e: g.scalar.activation(out[0], a[0], func, bias=val(bias), scale=scale), {"S": vec(a)})
         else:
-            run("S", [out, acc], [a, bias], lambda: g.scalar.activation(out[0], a[0], func, bias=val(bias), scale=scale, accum_out=acc[0]))
+            run([out, acc], [a, bias], lambda e: g.scalar.activation(out[0], a[0], func, bias=val(bias), scale=scale, accum_out=acc[0]), {"S": vec(a) + 20})
 
-    def cp(out, a, e="V"):
-        if e == "V":
-            run("V", [out], [a], lambda: g.vector.tensor_copy(out[0], a[0]))
-        else:
-            run("S", [out], [a], lambda: g.scalar.activation(out[0], a[0], AF.Copy))
+    def cp(out, a, es="V"):
+        def call(e):
+            if e == "V":
+                return g.vector.tensor_copy(out[0], a[0])
+            return g.scalar.activation(out[0], a[0], AF.Copy)
+        run([out], [a], call, {e: vec(a) for e in es})
 
     def fill(out, c):
-        run("V", [out], [], lambda: g.vector.memset(out[0], c))
+        run([out], [], lambda e: g.vector.memset(out[0], c), {"V": vec(out)})
 
     def red(out, a, op, ab=False):
-        run("V", [out], [a], lambda: g.vector.tensor_reduce(out[0], a[0], AxisListType.X, op, apply_absolute_value=ab))
+        run([out], [a], lambda e: g.vector.tensor_reduce(out[0], a[0], AxisListType.X, op, apply_absolute_value=ab), {"V": vec(a)})
 
     def turn(out, a):
-        run("V", [out], [a], lambda: g.vector.transpose(out[0], a[0]))
+        run([out], [a], lambda e: g.vector.transpose(out[0], a[0]), {"V": vec(a)})
 
     def scan(z, q):
         s = v("sm")
-        run("V", [z], [q, s], lambda: g.vector.tensor_tensor_scan(z[0], s[0], q[0], 0.0, OP.mult, OP.add))
+        run([z], [q, s], lambda e: g.vector.tensor_tensor_scan(z[0], s[0], q[0], 0.0, OP.mult, OP.add), {"V": vec(q)})
 
     def quant(q, s, a):
-        run("V", [q, s], [a], lambda: g.vector.quantize_mx(q[0], s[0], a[0]))
+        run([q, s], [a], lambda e: g.vector.quantize_mx(q[0], s[0], a[0]), {"V": 12 + 0.22 * a[7]})
 
     def mm(out, a, asc, b, bsc, start=True, stop=True):
-        run("T", [out], [a, asc, b, bsc], lambda: g.tensor.matmul_mx(out[0], a[0], asc[0], b[0], bsc[0], start, stop))
+        run([out], [a, asc, b, bsc], lambda e: g.tensor.matmul_mx(out[0], a[0], asc[0], b[0], bsc[0], start, stop), {"T": TENS})
 
-    def gather(out, win, off, e="V"):
-        run(e, [out], [win, off], (lambda: g.vector.tensor_copy(out[0], win[0].indirect(off[0]))) if e == "V"
-            else (lambda: g.scalar.activation(out[0], win[0].indirect(off[0]), AF.Copy)))
+    def by_list(out):
+        return 60 + 1.25 * out[7]
+
+    def gather(out, win, off, es="S", func=AF.Copy, scale=1.0, bias=0.0):
+        def call(e):
+            if e == "V":
+                return g.vector.tensor_copy(out[0], win[0].indirect(off[0]))
+            if func == AF.Copy:
+                return g.scalar.activation(out[0], win[0].indirect(off[0]), AF.Copy)
+            return g.scalar.activation(out[0], win[0].indirect(off[0]), func, bias=bias, scale=scale)
+        run([out], [win, off], call, {e: by_list(out) for e in es})
+
+    def choose(out, win, off, m):
+        run([out], [win, off, m], lambda e: g.vector.tensor_tensor(out[0], win[0].indirect(off[0]), m[0], OP.mult), {"V": by_list(out)})
 
     def pick(oq, os, oa, ob, iq, isc, ia, ib, off):
         o, w = v(oq, oa, ob), v(iq, ia, ib)
-        run("V", [o], [w, off], lambda: g.vector.tensor_copy(o[0].bitcast(dt.uint32), w[0].bitcast(dt.uint32).indirect(off[0])))
-        gather(v(os, oa, ob), v(isc, ia, ib), off, "S")
+        run([o], [w, off], lambda e: g.vector.tensor_copy(o[0].bitcast(dt.uint32), w[0].bitcast(dt.uint32).indirect(off[0])), {"V": by_list(o)})
+        gather(v(os, oa, ob), v(isc, ia, ib), off)
 
     def iota(out, pattern, base, cm, flag=True):
-        run("G", [out], [], lambda: g.iota(out[0], pattern, base, cm, allow_small_or_imprecise_dtypes=True) if flag else g.iota(out[0], pattern, base, cm))
+        run([out], [], lambda e: g.iota(out[0], pattern, base, cm, allow_small_or_imprecise_dtypes=True) if flag else g.iota(out[0], pattern, base, cm),
+            {"G": 130 + 1.66 * out[7]})
 
-    def quarters(name, c0, st, mid=None):
-        for e, d in (("V", 0), ("S", 1), ("V", 2), ("S", 3)):
+    def quarters(name, c0, st):
+        for d in range(4):
             a = d ^ 1
-            cp(v(name, 32 * a + c0, 32 * a + 32, st, 32 * d, 32 * d + 32), v(name, 32 * a + c0, 32 * a + 32, st, 32 * a, 32 * a + 32), "S" if mid else e)
-        if mid:
-            mid()
-        cp(v(name, 64 + c0, 128, st, 0, 64), v(name, 64 + c0, 128, st, 64, 128), "V")
-        cp(v(name, c0, 64, st, 64, 128), v(name, c0, 64, st, 0, 64), "S")
+            cp(v(name, 32 * a + c0, 32 * a + 32, st, 32 * d, 32 * d + 32), v(name, 32 * a + c0, 32 * a + 32, st, 32 * a, 32 * a + 32), "VS")
+        cp(v(name, 64 + c0, 128, st, 0, 64), v(name, 64 + c0, 128, st, 64, 128), "VS")
+        cp(v(name, c0, 64, st, 64, 128), v(name, c0, 64, st, 0, 64), "VS")
 
-    def wrap(tag, col, mid):
+    def wrap(tag, col):
         ts(v("qz" + tag), v("wm"), col, OP.mult)
         turn(v("qt" + tag), v("qz" + tag))
         scan(v("qs" + tag), v("qt" + tag))
-        quarters("qs" + tag, 15, 16, mid)
+        quarters("qs" + tag, 15, 16)
         return v("qs" + tag, 15, 128, 16)
 
     def ic(k):
@@ -194,65 +284,69 @@ def rank_program(g, core, T, topo):
     def fc(k):
         return v("fcol", k, k + 1)
 
-    dma("Y", "d_nbt", v("nbt", 0, 3), T.nb[:, :])
-    dma("S", "d_x", v("xt", 0, 512), T.x[:, :])
-    dma("Y", "d_nbr", v("nbr", 0, 384, 1, 0, 1), T.nb[:, :])
-    dma("Y", "d_w", v("wt", 0, 512), T.w[:, :])
+    classes = ((2, 0, 5), (1, 5, 5), (0, 10, 6))
+    dma("Y", "d_nbt", *[(v("nbt", 2 - (2 - i) % 3, 5 - (2 - i) % 3, 1, 8 * s, 8 * (s + n)), T.nb[i:16:3, :]) for i, s, n in classes])
+    dma("S", "d_x", (v("xt", 0, 512), T.x[:, :]))
+    for k, by in ((0, 6), (1, 11), (2, 0)):
+        moves = []
+        for h in range(2):
+            for i, s, n in classes:
+                p, c = 16 * h + (s + by) % 16, (k - i) % 3
+                moves.append((v("nl", 24 * k, 24 * k + 22, 1, p, p + n), T.nb[i:16:3, c:c + 22]))
+        dma("Y", "d_n%d" % k, *moves)
+    dma("Y", "d_w", (v("wt", 0, 512), T.w[:, :]))
 
     iota(ic(0), [[0, 1]], 0, 1, False)
-    iota(v("cc3", 0, 3), [[1, 3]], 0, 0)
-    iota(v("npi"), [[1, 128]], 128, -1, False)
     iota(v("npf"), [[1, 128]], 0, -1)
-    iota(v("n16"), [[0, 8], [1, 16]], 0, 0)
     iota(v("k128"), [[0, 128]], 128, 0)
-    iota(v("d8"), [[1, 8]], 0, 0)
+    iota(v("n16"), [[0, 8], [1, 16]], 0, 0)
+    iota(fc(0), [[0, 1]], 0, 1)
+    iota(v("d24"), [[1, 24]], 0, 0)
+    iota(fc(6), [[0, 1]], -64, 256)
+    iota(v("lf"), [[0, 32]], 0, 0)
+    iota(v("ks"), [[1, 4], [0, 128]], 0, 0)
+    iota(v("nbp"), [[0, 384]], 0, 0)
+    iota(v("pa", 0, 128), [[0, 128]], -1, 0)
     fill(v("et"), 0.0)
+    fill(v("mq"), -BIG)
     ts(ic(1), ic(0), 3, OP.arith_shift_right)
     ts(ic(2), ic(0), 7, OP.bitwise_and)
-    ts(ic(6), ic(0), 16 * r, OP.bitwise_and)
-    cp(fc(3), ic(0))
-    ts(ic(3), ic(1), 11, OP.mult)
-    ts(fc(0), ic(1), -5, OP.mult, 10, OP.add)
-    ts(fc(1), ic(1), -1, OP.mult, 2, OP.add)
-    ts(ic(4), ic(3), 5, OP.arith_shift_right)
-    ts(fc(4), ic(6), -2, OP.mult, fc(3), OP.add)
-    tt(ic(5), ic(2), ic(4), OP.add)
-    ts(fc(2), ic(4), 3, OP.mult, fc(1), OP.add)
-    ts(v("mk2", 0, 3), v("cc3", 0, 3), fc(2), OP.is_equal)
-    ts(fc(5), ic(5), 16, OP.mult, fc(0), OP.add)
-    ts(fc(6), fc(5), 128 * r, OP.add)
-    ts(fc(7), fc(5), 128 * 127, OP.add)
-    ts(fc(8), fc(4), 16 * r, OP.add, 256, OP.mult)
-    ts(v("npa"), v("npi"), 15, OP.bitwise_and)
-    ts(v("wm"), v("npa"), 0, OP.is_equal)
+    ts(ic(3), ic(0), 15, OP.bitwise_and)
+    cp(fc(1), ic(1))
+    cp(fc(2), ic(3))
+    ts(fc(3), ic(2), 16, OP.mult, fc(1), OP.add)
+    ts(fc(7), fc(2), 8, OP.mult)
+    ts(fc(4), fc(3), 128 * r, OP.add)
+    ts(fc(5), fc(3), 128 * 127 - 64, OP.add)
     act(v("npb"), v("npf"), AF.Abs)
-    act(v("sm"), v("n16"), AF.Sign)
     act(v("eye"), v("npb"), AF.Relu, -1.0, 1.0)
     act(v("et", 4, 516, 4), v("eye"), AF.Copy, 0.5)
+    for b in range(4):
+        quant(v("eq", 128 * b, 128 * b + 128), v("es", 128 * b, 128 * b + 128), v("et", 4 - b, 516 - b))
+    act(v("sm"), v("n16"), AF.Sign)
+    ts(v("wm"), v("n16"), fc(2), OP.is_equal)
 
-    tt(v("n2m", 0, 3), v("nbt", 0, 3), v("mk2", 0, 3), OP.mult)
-    red(ic(8), v("n2m", 0, 3), OP.max)
-    ts(ic(9), ic(8), 896, OP.bitwise_and)
-    ts(fc(9), ic(8), 0.5, OP.add, fc(6), OP.min)
-    ts(fc(10), ic(9), 8, OP.mult, fc(9), OP.add)
-    ts(v("zk"), v("npf"), 0.0, OP.mult, fc(10), OP.add)
+    ts(fc(9), v("nbt", 2, 3), 0.5, OP.add, fc(4), OP.min)
+    key = fc(9)
+    turned = [(k, bit, sign) for k, bit, sign in ((8, 128 * r, -8), (9, 896 - 128 * r, 8)) if bit]
+    for k, bit, sign in turned:
+        ts(ic(k), v("nbt", 2, 3), bit, OP.bitwise_and)
+    for k, bit, sign in turned:
+        ts(fc(k + 20), ic(k), sign, OP.mult, key, OP.add)
+        key = fc(k + 20)
+    ts(v("zk"), v("k128"), 0.0, OP.mult, key, OP.add)
     turn(v("rk"), v("zk"))
     quarters("rk", 0, 1)
-    act(v("sgn"), v("rk"), AF.Sign, -1.0, fc(10), fc(11))
-    nb1, nball = v("nbr", 0, 384, 1, 0, 1), v("nbb")
-    run("G", [nball], [nb1], lambda: g.partition_broadcast(nball[0], nb1[0], 128))
-    iota(v("ir"), [[1, 128]], 0, 0)
-    iota(v("ks"), [[1, 4], [0, 128]], 0, 0)
-    for t in "01":
-        fill(v("mb" + t, 1, 32), 0.0)
-        fill(v("my" + t), 0.0)
-        fill(v("tq" + t, 0, 1), 0.0)
-    ts(v("zx"), v("k128"), fc(11), OP.mult, fc(7), OP.add)
+    act(v("sgn"), v("rk"), AF.Sign, -1.0, key, fc(11))
+    ts(v("cl", 0, 8), v("d24", 0, 8), fc(7), OP.add)
+    quant(v("q0"), v("q0s"), v("xt", 0, 512))
+    ts(v("zx"), v("k128"), fc(11), OP.mult, fc(5), OP.add)
     turn(v("rx"), v("zx"))
     quarters("rx", 0, 1)
-    ts(v("dx"), v("rx"), fc(8), OP.subtract)
+    ts(v("dx"), v("rx"), fc(6), OP.subtract)
     red(fc(12), v("dx"), OP.min, True)
-    wp = wrap("p", fc(12), lambda: quant(v("q0"), v("q0s"), v("xt", 0, 512)))
+    gather(v("posn"), v("rx"), v("cl", 0, 8), "S", AF.Identity, 1.0 / 256, WHOLE)
+    wp = wrap("p", fc(12))
     cp(v("pl", 0, 8), wp)
     pick("w0", "ws0", 0, 128, "q0", "q0s", 0, 128, v("pl", 0, 8))
 
@@ -262,16 +356,14 @@ def rank_program(g, core, T, topo):
     near = [(d, c) for d, c in peers if c in chip]
     lanes = topo.engines(core, far[0][1])
     spare = 2 * len(far) - len(lanes)
+    inside = [e for e in topo.engines(core, near[0][1]) if e not in lanes][:2]
     ways = []
     for part in range(2):
         mine = lanes[spare:] + lanes[:spare] if part else lanes
-        way = {}
+        way = {d: inside for d, c in near}
         for k, (d, c) in enumerate(far):
             way[d] = [mine[k]] if k < spare else [mine[spare + 2 * (k - spare)], mine[spare + 2 * (k - spare) + 1]]
-        for d, c in near:
-            way[d] = [e for e in topo.engines(core, c) if e not in lanes][:2]
         ways.append(way)
-    arrive = sum(len(x) for w in ways for x in w.values())
 
     def bits(es):
         return sum(1 << e for e in es)
@@ -280,27 +372,34 @@ def rank_program(g, core, T, topo):
         rid, pid = topo.addr(c, core)
         return DstId(rid=rid, pnc=pid)
 
+    def post(src, tr, leave, land):
+        def emit(e):
+            order("G", [], [src])
+            g.remote_dma_fused(tr, local_sem=T.sem.sent)
+            total["sent"] = total.get("sent", 0) + leave
+        i = add([], [src], emit, {"G": ISSUE})
+        add([land], [], None, {"R": 0.0}, FLIGHT, (i,))
+
     def send(t, part):
         name, dst = (("w" + t, "land" + t), ("ws" + t, "lands" + t))[part]
-        order("G", [], [v(name, 16, 128)])
         tr = []
         for d, c in peers:
             a, b = T[name][:, 16 * d:16 * d + 16], T[dst][:, 16 * d:16 * d + 16]
             if part == 0:
                 a, b = a.bitcast(dt.uint8), b.bitcast(dt.uint8)
             tr.append(RemoteDMATransfer(dst_ids=[dest(c)], dma_engine_mask=bits(ways[part][d]), remote_sem=T.sem["arr" + t], src=a, dst=b))
-        g.remote_dma_fused(tr, local_sem=T.sem.sent)
-        total["sent"] = total.get("sent", 0) + sum(len(x) for x in ways[part].values())
+        post(v(name, 0, 128), tr, sum(len(x) for x in ways[part].values()), v(dst, 16, 128))
 
     def send_best(t):
-        order("G", [], [v("mb" + t, 0, 1)])
-        tr = RemoteDMATransfer(dst_ids=[dest(c) for d, c in peers], dma_engine_mask=bits(lanes), remote_sem=T.sem["thr" + t],
-                               srcs=[T["mb" + t][:, 0:1]], dsts=[T["lt" + t][:, d:d + 1] for d, c in peers])
-        g.remote_dma_fused([tr], local_sem=T.sem.sent)
-        total["sent"] = total.get("sent", 0) + len(lanes)
+        c0, tr = 32 * int(t), []
+        for who, es in ((far, lanes), (near, inside)):
+            tr.append(RemoteDMATransfer(dst_ids=[dest(c) for d, c in who], dma_engine_mask=bits(es), remote_sem=T.sem["thr" + t],
+                                        srcs=[T.mq[:, c0:c0 + 1]], dsts=[T["lt" + t][:, d:d + 1] for d, c in who]))
+        post(v("mq", c0, c0 + 1), tr, len(lanes) + len(inside), v("lt" + t, 1, 8))
 
     for t in "01":
-        total["arr" + t], total["thr" + t] = arrive, (N - 1) * len(lanes)
+        total["arr" + t] = sum(len(x) for w in ways for x in w.values())
+        total["thr" + t] = len(far) * len(lanes) + len(near) * len(inside)
         note("R", [v("land" + t, 16, 128), v("lands" + t, 16, 128)], [], ("arr" + t, total["arr" + t]))
         note("R", [v("lt" + t, 1, 8)], [], ("thr" + t, total["thr" + t]))
 
@@ -317,149 +416,143 @@ def rank_program(g, core, T, topo):
                 act(x, x, AF.Identity, bias=v("pen1", col, col + 1), acc=out)
 
     def halves(t, k, part):
+        a = 128 * k
+        if part == 0:
+            m, s = v("w" + t, 0, 128), v("ws" + t, 0, 128)
+        elif k == 2:
+            m, s = v("land" + t), v("lands" + t)
+        else:
+            m, s = v("g" + t, a, a + 128), v("gs" + t, a, a + 128)
         for b in range(4):
-            o, e, es = v("pn", 512 * b, 512 * b + 128), v("eq", 128 * b, 128 * b + 128), v("es", 128 * b, 128 * b + 128)
-            if part == 0:
-                mm(o, e, es, v("w" + t, 0, 128), v("ws" + t, 0, 128), True, False)
-            elif k < 2:
-                mm(o, e, es, v("g" + t, 128 * k, 128 * k + 128), v("gs" + t, 128 * k, 128 * k + 128), False, True)
-            else:
-                mm(o, e, es, v("land" + t), v("lands" + t), False, True)
+            mm(v("pn", 512 * b, 512 * b + 128), v("eq", 128 * b, 128 * b + 128), v("es", 128 * b, 128 * b + 128), m, s, part == 0, part == 1)
 
     def drain(t, k):
         for b in range(4):
-            cp(v("nt" + t, 512 * k + b, 512 * k + 512, 4), v("pn", 512 * b, 512 * b + 128), "S")
+            cp(v("nt" + t, 512 * k + b, 512 * k + 512, 4), v("pn", 512 * b, 512 * b + 128), "VS")
 
     def requant(t, k):
-        quant(v("w" + t, 128 * k + 128, 128 * k + 256), v("ws" + t, 128 * k + 128, 128 * k + 256), v("nt" + t, 512 * k, 512 * k + 512))
+        a = 128 * k + 128
+        quant(v("w" + t, a, a + 128), v("ws" + t, a, a + 128), v("nt" + t, 512 * k, 512 * k + 512))
 
     for t in "01":
         W, WS, G, GS, L, LS, sc, met = "w" + t, "ws" + t, "g" + t, "gs" + t, "land" + t, "lands" + t, "sc" + t, "met" + t
 
-        def s_(a, b=None):
-            return v(sc, a, a + 1 if b is None else b)
+        def s_(a):
+            return v(sc, a, a + 1)
 
         def m_(a):
             return v(met, a, a + 1)
 
+        mb, mx = 32 * int(t), "mx" + t
+        best = v("mq", mb, mb + 1)
         send(t, 0)
         send(t, 1)
         mm(bank(0), v(W, 0, 128), v(WS, 0, 128), v(W, 0, 128), v(WS, 0, 128))
         if t == "0":
-            for k in range(3):
-                ts(v("tli", 8 * k, 8 * k + 8), wp, 3, OP.mult, k, OP.add)
-            ts(v("tla"), v("tli"), 15, OP.bitwise_and)
-            ts(v("tlb"), v("tli"), 4, OP.arith_shift_right)
-            ts(fc(13), fc(12), 128 * r, OP.add)
-            ts(v("tlc"), v("tla"), 24, OP.mult)
-            tt(v("tla"), v("tlc"), v("tlb"), OP.add)
-            cp(v("tl"), v("tla"))
-            gather(v("prw", 128, 384), v("nbb"), v("tl", 0, 16))
+            ts(v("lf", 0, 24, 1, 0, 32), v("nl", 0, 72, 3, 0, 32), 0, OP.add)
+            cp(v("lf", 0, 16, 1, 32, 64), v("lf", 0, 16, 1, 0, 32), "S")
+            cp(v("lf", 0, 16, 1, 64, 128), v("lf", 0, 16, 1, 0, 64), "S")
+            ts(v("nlu", 0, 16), v("lf", 0, 16), -128 * r, OP.add)
+            gather(v("npos"), v("posn"), v("nlu", 0, 16), "S", AF.Identity, 1.0, -WHOLE)
+            ts(v("pl", 8, 16), wp, 128, OP.add)
+            gather(v("nsl"), v("npos"), v("pl", 0, 16))
             for k in range(2):
-                ts(v("e%d" % k), v("prw", 128 * k + 128, 128 * k + 256), fc(13), OP.is_equal)
-        else:
-            pick("o1", "o1s", 0, 128, W, WS, 0, 128, v("pol", 0, 8))
-        scores(t, [(0, 0, "e0", 1), (1, 0, "e1", 0)])
-        best = v("mb" + t, 0, 1)
-        if t == "0":
-            out, off, src = v("posr"), v("pl", 0, 8), v("ir")
-            run("V", [out], [off, src], lambda: g.vector.tensor_copy(out[0].indirect(off[0]), src[0]))
-        tt(best, s_(0), s_(1), OP.max)
-        send_best(t)
-        if t == "0":
+                ts(v("e%d" % k), v("nsl", 128 * k, 128 * k + 128), fc(0), OP.is_equal)
             for k in range(2):
-                tt(v("xm%d" % k), v("prw", 128 * k + 128, 128 * k + 256), v("wm"), OP.mult)
+                choose(v("xm%d" % k), v("npos", 128 * k, 128 * k + 128), v("pl", 0, 8), v("wm"))
             for k in range(2):
                 scan(v("xs%d" % k), v("xm%d" % k))
             for k in range(2):
-                ts(v("xl", 8 * k, 8 * k + 8), v("xs%d" % k, 15, 128, 16), -128 * r, OP.add)
-            pick(G, GS, 0, 256, "q0", "q0s", 0, 128, v("xl", 0, 16))
-            for b in range(4):
-                quant(v("eq", 128 * b, 128 * b + 128), v("es", 128 * b, 128 * b + 128), v("et", 4 - b, 516 - b))
-            ts(ic(10), ic(0), 15, OP.bitwise_and)
-            ts(ic(11), ic(0), 1, OP.bitwise_and)
-            ts(ic(12), ic(0), 4, OP.arith_shift_right)
-            ts(fc(17), ic(11), -2, OP.mult, 1, OP.add)
-            cp(fc(18), ic(12))
-            ts(v("swl", 0, 1), ic(10), fc(17), OP.add)
-            ts(v("dm"), v("d8"), fc(18), OP.is_equal)
+                cp(v("xsl", 8 * k, 8 * k + 8), v("xs%d" % k, 15, 128, 16))
+            ts(ic(4), ic(0), 1, OP.bitwise_and)
+            ts(ic(5), ic(0), 4, OP.arith_shift_right)
+            ts(fc(13), ic(4), -2, OP.mult, fc(2), OP.add)
+            cp(fc(14), ic(5))
+            ts(v("swl", 0, 1), fc(13), 1, OP.add)
+            ts(v("dmb"), v("d24", 0, 8), fc(14), OP.not_equal, BIG, OP.mult)
         else:
-            pick(G, GS, 0, 256, "o1", "o1s", 0, 128, v("xl", 0, 16))
-        mm(bank(1), v(G, 0, 128), v(GS, 0, 128), v(G, 128, 256), v(GS, 128, 256))
-        mm(bank(2), v(G, 128, 256), v(GS, 128, 256), v(G, 0, 128), v(GS, 0, 128))
-        pick(L, LS, 0, 16, W, WS, 0, 128, v("swl", 0, 1))
+            ts(v("pen1", 0, 2), v("met0", 0, 2), -BIG / 128, OP.mult)
+            ts(v("pen1", 4, 5), v("met0", 2, 3), -BIG / 128, OP.mult)
+        scores(t, [(0, 0, "e0", 0), (1, 0, "e1", 1)])
+        tt(best, s_(0), s_(1), OP.max)
+        send_best(t)
+        pick(G, GS, 0, 256, W, WS, 0, 128, v("xsl", 0, 16))
         halves(t, 0, 0)
         halves(t, 0, 1)
+        pick(L, LS, 0, 16, W, WS, 0, 128, v("swl", 0, 1))
+        mm(bank(2), v(G, 0, 128), v(GS, 0, 128), v(G, 128, 256), v(GS, 128, 256))
+        mm(bank(3), v(G, 128, 256), v(GS, 128, 256), v(G, 0, 128), v(GS, 0, 128))
         if t == "1":
-            gather(v("selr"), v("ks"), v("vl0"), "S")
             for k in range(2):
                 x = v("selm", 128 * k, 128 * k + 128)
-                tt(x, v("selr"), v("e%d" % k), OP.mult)
+                choose(x, v("ks"), v("vl0"), v("e%d" % k))
                 act(x, x, AF.Copy, acc=fc(20 + k))
-            for col, who, k in ((2, 20, 2), (3, 21, 1), (5, 20, 3), (6, 21, 3)):
-                ts(v("pen1", col, col + 1), fc(who), k, OP.is_equal, -BIG / 128, OP.mult)
-        scores(t, [(2, 1, "e0", 2), (3, 2, "e1", 3)])
+            ts(v("pen1", 2, 3), fc(20), 2, OP.is_equal, -BIG / 128, OP.mult)
+            ts(v("pen1", 3, 4), fc(21), 1, OP.is_equal, -BIG / 128, OP.mult)
+            ts(v("pen1", 5, 7), v("fcol", 20, 22), 3, OP.is_equal, -BIG / 128, OP.mult)
         drain(t, 0)
         halves(t, 1, 0)
         halves(t, 1, 1)
-        turn(v("mx" + t, 0, 32, 1, 0, 32), v("mb" + t, 0, 32, 1, 0, 32))
-        cp(v("my" + t, 0, 16, 2, 0, 32), v("mx" + t, 1, 16, 2, 0, 32))
-        cp(v("my" + t, 1, 16, 2, 0, 32), v("mx" + t, 0, 16, 2, 0, 32))
-        turn(v("mz" + t, 0, 32, 1, 0, 32), v("my" + t, 0, 32, 1, 0, 32))
-        cp(v("tq" + t, 0, 1, 1, 0, 32), v("mz" + t, 0, 1, 1, 0, 32))
-        tt(s_(8, 10), s_(0, 2), s_(2, 4), OP.max)
-        ts(s_(10), s_(8), s_(1), OP.is_gt, -9 * BIG, OP.mult)
-        ts(s_(11), s_(9), s_(0), OP.is_ge, -9 * BIG, OP.mult)
-        tt(s_(12), s_(10), s_(1), OP.add)
-        tt(s_(13), s_(11), s_(0), OP.add)
+        scores(t, [(2, 2, "e0", 2), (3, 3, "e1", 3)])
         requant(t, 0)
+        turn(v(mx, 0, 32, 1, 0, 32), v("mq", mb, mb + 32, 1, 0, 32))
+        cp(v("mq", 64, 80, 2, 0, 32), v(mx, 1, 16, 2, 0, 32), "VS")
+        cp(v("mq", 65, 80, 2, 0, 32), v(mx, 0, 16, 2, 0, 32), "VS")
+        turn(v("mq", 96, 128, 1, 0, 32), v("mq", 64, 96, 1, 0, 32))
+        ts(s_(10), s_(1), s_(2), OP.max, s_(0), OP.is_gt)
+        ts(s_(11), s_(0), s_(3), OP.max, s_(1), OP.is_ge)
+        tt(s_(7), v("mq", 96, 97), best, OP.max)
+        ts(s_(12), s_(10), -9 * BIG, OP.mult, s_(0), OP.add)
+        ts(s_(13), s_(11), -9 * BIG, OP.mult, s_(1), OP.add)
         drain(t, 1)
-        requant(t, 1)
         halves(t, 2, 0)
+        requant(t, 1)
         if t == "0":
-            tt(v("posm"), v("posr"), v("wm"), OP.mult)
-            scan(v("poss"), v("posm"))
-            cp(v("pol", 0, 8), v("poss", 15, 128, 16))
+            turn(v("lft", 0, 32, 1, 0, 32), v("lf", 0, 32, 1, 0, 32))
+            dma("Y", "d_nbp", (v("nbp", 0, 384, 1, 0, 1), v("lft", 0, 16, 1, 0, 24)))
         else:
-            fill(v("prw", 0, 128), -1.0)
-            gather(v("prw", 384, 512), v("nbb"), v("tl", 16, 24))
-            gather(v("prs0"), v("prw"), v("vl0"), "S")
-            gather(v("pro0"), v("prs0"), v("pol", 0, 8), "S")
-            dma("Y", "d_p0", T.pr[0:1, :], v("pro0", 0, 128, 1, 0, 1))
+            ts(v("pl", 16, 24), wp, 256, OP.add)
+            tt(v("posm"), v("posn"), v("wm"), OP.mult)
+            gather(v("pa", 128, 512), v("nbp"), v("pl"), "VS")
+            scan(v("poss"), v("posm"))
+            ts(v("pol", 0, 8), v("poss", 15, 128, 16), -WHOLE, OP.add)
             quant(v("wq"), v("wqs"), v("wt", 0, 512))
+            gather(v("prs0"), v("pa"), v("vl0"), "VS")
+            gather(v("pro0"), v("prs0"), v("pol", 0, 8), "VS")
+            dma("Y", "d_p0", (T.pr[0:1, :], v("pro0", 0, 128, 1, 0, 1)))
         mm(bank(0), v(W, 0, 128), v(WS, 0, 128), v(L), v(LS))
         mm(bank(1), v(G, 0, 128), v(GS, 0, 128), v(L), v(LS))
         mm(bank(2), v(G, 128, 256), v(GS, 128, 256), v(L), v(LS))
         halves(t, 2, 1)
         scores(t, [(4, 0, "eye", 4), (5, 1, "e0", 5), (6, 2, "e1", 6)])
-        drain(t, 2)
-        tt(v("tq" + t, 1, 8), v("lt" + t, 1, 8), v("dm", 1, 8), OP.mult)
-        red(s_(14), v("tq" + t), OP.add)
-        ts(m_(2), s_(14), best, OP.max, s_(4), OP.is_lt)
+        ts(v("s4m" + t, 1, 8), v("dmb", 1, 8), s_(4), OP.add)
+        ts(v("cq" + t, 0, 1), s_(7), s_(4), OP.is_lt)
         ts(m_(0), s_(5), s_(4), OP.max, s_(12), OP.is_le)
-        ts(s_(15), m_(2), 384, OP.mult, fc(3), OP.add)
         ts(m_(1), s_(6), s_(4), OP.max, s_(13), OP.is_le)
-        ts(s_(16), m_(0), 128, OP.mult, s_(15), OP.add)
-        ts(s_(18), m_(1), 256, OP.mult, s_(16), OP.add)
-        wv = wrap("v" + t, s_(18), lambda: requant(t, 2))
-        cp(v("vl" + t), wv)
+        ts(s_(15), m_(0), 128, OP.mult, fc(0), OP.add)
+        ts(s_(16), m_(1), 256, OP.mult, s_(15), OP.add)
+        drain(t, 2)
+        tt(v("cq" + t, 1, 8), v("lt" + t, 1, 8), v("s4m" + t, 1, 8), OP.is_lt)
+        red(m_(2), v("cq" + t), OP.min)
+        ts(s_(18), m_(2), 384, OP.mult, s_(16), OP.add)
+        requant(t, 2)
+        cp(v("vl" + t), wrap("v" + t, s_(18)))
         if t == "0":
             pick("w1", "ws1", 0, 128, W, WS, 0, 512, v("vl0"))
-            for k, col in ((1, 0), (0, 1), (2, 4)):
-                ts(v("pen1", col, col + 1), m_(k), -BIG / 128, OP.mult)
 
     pick("f0", "f0s", 0, 128, "w1", "ws1", 0, 512, v("vl1"))
     pick("f1", "f1s", 0, 128, "f0", "f0s", 0, 128, v("pol", 0, 8))
     mm(bank(3), v("wq"), v("wqs"), v("f1"), v("f1s"))
     f1 = v("f1")
-    dma("Y", "d_oc", T.oc[:, :], (T.f1[:, :].bitcast(dt.uint8),) + f1[1:])
-    gather(v("prs1"), v("prw"), v("vl1"), "S")
-    gather(v("pro1"), v("prs1"), v("pol", 0, 8), "S")
-    cp(v("yo"), bank(3))
+    dma("Y", "d_oc", (T.oc[:, :], (T.f1[:, :].bitcast(dt.uint8),) + f1[1:]))
+    gather(v("prs1"), v("pa"), v("vl1"), "VS")
+    gather(v("pro1"), v("prs1"), v("pol", 0, 8), "VS")
+    cp(v("yo"), bank(3), "VS")
     for k in range(4):
-        dma("Y" if k < 2 else "S", "d_os%d" % k, T.osc[4 * k:4 * k + 4, :], v("f1s", 0, 128, 1, 32 * k, 32 * k + 4))
-    dma("Y", "d_y", T.y[:, :], v("yo"))
-    dma("S", "d_p1", T.pr[1:2, :], v("pro1", 0, 128, 1, 0, 1))
+        dma("Y", "d_os%d" % k, (T.osc[4 * k:4 * k + 4, :], v("f1s", 0, 128, 1, 32 * k, 32 * k + 4)))
+    dma("S", "d_y", (T.y[:, :], v("yo")))
+    dma("Y", "d_p1", (T.pr[1:2, :], v("pro1", 0, 128, 1, 0, 1)))
+    schedule()
     for sem, n in total.items():
         if waited.get(sem, 0) < n:
             (g if sem == "sent" else g.sync).wait_ge(T.sem[sem], n)

@@ -14,48 +14,98 @@ _declare(I32, 72, "nl")
 _declare(I32, 16, "icol")
 _declare(I32, 8, "nbt")
 _declare(BF16, 520, "xt wt et")
-_declare(BF16, 128, "sgn")
+_declare(BF16, 128, "sgn wmb wmh smb")
+_declare(BF16, 8, "dmk dsr dt1 dxm")
 _declare(F32, 64, "fcol")
 _declare(F32, 24, "d24")
-_declare(F32, 32, "lf lft")
+_declare(F32, 32, "lf lft pq pqt")
 _declare(F32, 8, "dmb")
-_declare(F32, 128, "mq npf npb n16 k128 wm sm eye zk rk zx rx dx e0 e1 posn posm poss yo xm0 xm1 xs0 xs1")
+_declare(F32, 128, "mq npf npb n16 k128 wm nmA nmB nm ed zz sm eye zk rk zx rx dx e0 e1 posn yo xm0 xm1 xs0 xs1")
 _declare(F32, 256, "selm npos nsl")
-_declare(F32, 384, "nbp")
+_declare(F32, 384, "nbp pb")
 _declare(F32, 512, "ks pa")
-_declare(U16, 24, "nlu pl swl cl xsl pol")
+_declare(U16, 24, "nlu pl swl cl xsl pol gll dll")
 _declare(C4, 512, "eq")
 _declare(U8, 512, "es")
-_declare(C4, 128, "q0 wq f0 f1")
-_declare(U8, 128, "q0s wqs f0s f1s")
-for _c in ("p", "v0", "v1"):
-    _declare(F32, 128, "qz%s qt%s qs%s" % (_c, _c, _c))
+_declare(C4, 256, "ll")
+_declare(U8, 256, "lls")
+_declare(U8, 128, "hls")
+_declare(C4, 128, "q0 wq f0 f1 gl l1")
+_declare(U8, 128, "q0s wqs f0s f1s gls l1s")
+for _c in ("p", "v0", "v1", "l", "d"):
+    _declare(BF16, 128, "qz%s qt%s qs%s" % (_c, _c, _c))
 for _t in "01":
     _declare(C4, 512, "w" + _t)
     _declare(U8, 512, "ws" + _t)
     _declare(C4, 256, "g" + _t)
     _declare(U8, 256, "gs" + _t)
-    _declare(C4, 128, "land" + _t)
-    _declare(U8, 128, "lands" + _t)
     _declare(F32, 8, "lt%s cq%s s4m%s pen%s met%s" % (_t, _t, _t, _t, _t))
     _declare(F32, 32, "mx%s sc%s" % (_t, _t))
     _declare(F32, 1024, "ex" + _t)
     _declare(BF16, 1536, "nt" + _t)
     _declare(U16, 8, "vl" + _t)
     _declare(F32, 128, "prs%s pro%s" % (_t, _t))
-DMAS = ["d_nbt", "d_n0", "d_n1", "d_n2", "d_x", "d_w", "d_nbp", "d_oc", "d_os0", "d_os1", "d_os2", "d_os3", "d_y", "d_p0", "d_p1"]
-SEMAPHORES = ["cV", "cS", "cT", "cG", "sent", "arr0", "arr1", "thr0", "thr1"] + DMAS
+DMAS = ["d_nbt", "d_nbu", "d_n0", "d_n1", "d_n2", "d_x", "d_w", "d_nbp", "d_pq0", "d_pq1", "d_oc", "d_os0", "d_os1", "d_os2", "d_os3", "d_y", "d_p0", "d_p1"]
+SEMAPHORES = ["cV", "cS", "cT", "cG", "sent", "arr0", "arr1", "thr0", "thr1", "thd", "hop"] + DMAS
 BIG = 1e29
-WAKE, TENS, LOAD, ISSUE, FLIGHT = 100.0, 110.0, 1500.0, 600.0, 4500.0
+WAKE, TENS, LOAD, ISSUE, FLIGHT = 200.0, 130.0, 1000.0, 400.0, 3500.0
+HOP, WAY0, WAY1 = 2500.0, 4200.0, 3000.0
 LOOK = 250.0
 WHOLE = 12582912.0
 
 
 def rank_program(g, core, T, topo):
-    r = T.rank_of(core)
+    N, cores = len(T.cores), T.cores
+    owner, helper = {}, {}
+    for c in cores:
+        for h in topo.cores_of(c):
+            if h not in cores and h not in owner and topo.die(h) == topo.die(c) and all(topo.may_write(h, d) for d in cores):
+                owner[h], helper[c] = c, h
+                break
+    me = owner.get(core, core)
+    r = T.rank_of(me)
     if r is None:
         return
-    N, cores = len(T.cores), T.cores
+
+    peers = [(d, cores[r ^ d]) for d in range(1, N)]
+    chip = topo.cores_of(core)
+    far = [(d, c) for d, c in peers if c not in chip]
+    near = [(d, c) for d, c in peers if c in chip]
+    lanes = topo.engines(core, far[0][1])
+    spare = 2 * len(far) - len(lanes)
+    others = [e for e in topo.engines(core, near[0][1]) if e not in lanes]
+    inside = others[:2]
+    ways = []
+    for part in range(2):
+        mine = lanes[spare:] + lanes[:spare] if part else lanes
+        way = {d: inside for d, c in near}
+        for k, (d, c) in enumerate(far):
+            way[d] = [mine[k]] if k < spare else [mine[spare + 2 * (k - spare)], mine[spare + 2 * (k - spare) + 1]]
+        ways.append(way)
+    leave = [sum(len(x) for x in w.values()) for w in ways]
+
+    def bits(es):
+        return sum(1 << e for e in es)
+
+    def dest(c):
+        rid, pid = topo.addr(c, core)
+        return DstId(rid=rid, pnc=pid)
+
+    def columns(name, dst, c0, d0, part, sem):
+        tr = []
+        for d, c in peers:
+            a, b = T[name][:, c0 + 16 * d:c0 + 16 * d + 16], T[dst][:, d0 + 16 * d:d0 + 16 * d + 16]
+            if part == 0:
+                a, b = a.bitcast(dt.uint8), b.bitcast(dt.uint8)
+            tr.append(RemoteDMATransfer(dst_ids=[dest(c)], dma_engine_mask=bits(ways[part][d]), remote_sem=T.sem[sem], src=a, dst=b))
+        return tr
+
+    if core != me:
+        g.wait_ge(T.sem.hop, len(others))
+        g.remote_dma_fused(columns("hls", "lls", 0, 128, 1, "arr1"), local_sem=T.sem.sent)
+        g.wait_ge(T.sem.sent, leave[1])
+        return
+
     queue = {"V": g.vector, "S": g.scalar, "T": g.tensor, "G": g, "Y": g.sync}
     count = {e: 0 for e in "VSTG"}
     known = {e: {} for e in "VSTGY"}
@@ -132,7 +182,7 @@ def rank_program(g, core, T, topo):
             total[tok[0]] = count[e]
             snap[tok] = dict(known[e])
             note(e, outs, ins, tok)
-        add(outs, ins, emit, cost)
+        return add(outs, ins, emit, cost)
 
     def schedule():
         n = len(ops)
@@ -197,7 +247,7 @@ def rank_program(g, core, T, topo):
         add(outs, ins, emit, {e: 60.0 * len(moves)}, LOAD)
 
     def vec(x, a=1.0):
-        return max(64, a * x[7]) * 0.83
+        return max(64, a * x[7] * (0.5 if SCRATCH[x[1]][2] == BF16 else 1)) * 0.83
 
     def ts(out, a, s1, op0, s2=None, op1=None):
         if op1 is None:
@@ -210,7 +260,7 @@ def rank_program(g, core, T, topo):
 
     def act(out, a, func, scale=1.0, bias=0.0, acc=None):
         if acc is None:
-            run([out], [a, bias], lambda e: g.scalar.activation(out[0], a[0], func, bias=val(bias), scale=scale), {"S": vec(a)})
+            run([out], [a, bias, scale], lambda e: g.scalar.activation(out[0], a[0], func, bias=val(bias), scale=val(scale)), {"S": vec(a)})
         else:
             run([out, acc], [a, bias], lambda e: g.scalar.activation(out[0], a[0], func, bias=val(bias), scale=scale, accum_out=acc[0]), {"S": vec(a) + 20})
 
@@ -230,9 +280,9 @@ def rank_program(g, core, T, topo):
     def turn(out, a):
         run([out], [a], lambda e: g.vector.transpose(out[0], a[0]), {"V": vec(a)})
 
-    def scan(z, q):
-        s = v("sm")
-        run([z], [q, s], lambda e: g.vector.tensor_tensor_scan(z[0], s[0], q[0], 0.0, OP.mult, OP.add), {"V": vec(q)})
+    def scan(z, q, op=OP.add):
+        s = v("smb" if SCRATCH[q[1]][2] == BF16 else "sm")
+        run([z], [q, s], lambda e: g.vector.tensor_tensor_scan(z[0], s[0], q[0], 0.0, OP.mult, op), {"V": vec(q)})
 
     def quant(q, s, a):
         run([q, s], [a], lambda e: g.vector.quantize_mx(q[0], s[0], a[0]), {"V": 12 + 0.22 * a[7]})
@@ -257,8 +307,9 @@ def rank_program(g, core, T, topo):
 
     def pick(oq, os, oa, ob, iq, isc, ia, ib, off):
         o, w = v(oq, oa, ob), v(iq, ia, ib)
-        run([o], [w, off], lambda e: g.vector.tensor_copy(o[0].bitcast(dt.uint32), w[0].bitcast(dt.uint32).indirect(off[0])), {"V": by_list(o)})
+        i = run([o], [w, off], lambda e: g.vector.tensor_copy(o[0].bitcast(dt.uint32), w[0].bitcast(dt.uint32).indirect(off[0])), {"V": by_list(o)})
         gather(v(os, oa, ob), v(isc, ia, ib), off)
+        return i
 
     def iota(out, pattern, base, cm, flag=True):
         run([out], [], lambda e: g.iota(out[0], pattern, base, cm, allow_small_or_imprecise_dtypes=True) if flag else g.iota(out[0], pattern, base, cm),
@@ -272,11 +323,18 @@ def rank_program(g, core, T, topo):
         cp(v(name, c0, 64, st, 64, 128), v(name, c0, 64, st, 0, 64), "VS")
 
     def wrap(tag, col):
-        ts(v("qz" + tag), v("wm"), col, OP.mult)
+        ts(v("qz" + tag), v("wmh"), col, OP.mult)
         turn(v("qt" + tag), v("qz" + tag))
         scan(v("qs" + tag), v("qt" + tag))
         quarters("qs" + tag, 15, 16)
         return v("qs" + tag, 15, 128, 16)
+
+    def wrap_sum(tag, a, b, out):
+        ts(v("qz" + tag), v("wmb"), a, OP.add, b, OP.add)
+        turn(v("qt" + tag), v("qz" + tag))
+        scan(v("qs" + tag), v("qt" + tag), OP.max)
+        quarters("qs" + tag, 15, 16)
+        ts(out, v("qs" + tag, 15, 128, 16), 128, OP.mult, fc(17), OP.add)
 
     def ic(k):
         return v("icol", k, k + 1)
@@ -285,7 +343,9 @@ def rank_program(g, core, T, topo):
         return v("fcol", k, k + 1)
 
     classes = ((2, 0, 5), (1, 5, 5), (0, 10, 6))
-    dma("Y", "d_nbt", *[(v("nbt", 2 - (2 - i) % 3, 5 - (2 - i) % 3, 1, 8 * s, 8 * (s + n)), T.nb[i:16:3, :]) for i, s, n in classes])
+    part = [(v("nbt", 2 - (2 - i) % 3, 5 - (2 - i) % 3, 1, 8 * s, 8 * (s + n)), T.nb[i:16:3, :]) for i, s, n in classes]
+    dma("S", "d_nbu", part[0])
+    dma("Y", "d_nbt", *part[1:])
     dma("S", "d_x", (v("xt", 0, 512), T.x[:, :]))
     for k, by in ((0, 6), (1, 11), (2, 0)):
         moves = []
@@ -307,6 +367,8 @@ def rank_program(g, core, T, topo):
     iota(v("ks"), [[1, 4], [0, 128]], 0, 0)
     iota(v("nbp"), [[0, 384]], 0, 0)
     iota(v("pa", 0, 128), [[0, 128]], -1, 0)
+    iota(v("pb", 0, 128), [[0, 128]], -1, 0)
+    fill(v("zz"), 0.0)
     fill(v("et"), 0.0)
     fill(v("mq"), -BIG)
     ts(ic(1), ic(0), 3, OP.arith_shift_right)
@@ -325,16 +387,29 @@ def rank_program(g, core, T, topo):
         quant(v("eq", 128 * b, 128 * b + 128), v("es", 128 * b, 128 * b + 128), v("et", 4 - b, 516 - b))
     act(v("sm"), v("n16"), AF.Sign)
     ts(v("wm"), v("n16"), fc(2), OP.is_equal)
+    ts(v("wmb"), v("n16"), fc(2), OP.is_equal, 4, OP.mult)
+    ts(v("wmh"), v("n16"), fc(2), OP.is_equal)
+    cp(v("smb"), v("sm"), "S")
+    ts(ic(5), ic(0), 4, OP.arith_shift_right)
+    cp(fc(14), ic(5))
+    ts(fc(15), fc(14), 0.125, OP.mult)
+    ts(fc(16), fc(14), 0, OP.is_equal, fc(15), OP.add)
+    ts(fc(17), fc(2), -512, OP.add)
+    fill(v("pq", 0, 32, 1, 0, 32), 0.0)
 
     ts(fc(9), v("nbt", 2, 3), 0.5, OP.add, fc(4), OP.min)
-    key = fc(9)
     turned = [(k, bit, sign) for k, bit, sign in ((8, 128 * r, -8), (9, 896 - 128 * r, 8)) if bit]
     for k, bit, sign in turned:
         ts(ic(k), v("nbt", 2, 3), bit, OP.bitwise_and)
-    for k, bit, sign in turned:
-        ts(fc(k + 20), ic(k), sign, OP.mult, key, OP.add)
-        key = fc(k + 20)
-    ts(v("zk"), v("k128"), 0.0, OP.mult, key, OP.add)
+    k, bit, sign = turned[0]
+    ts(fc(28), ic(k), sign, OP.mult)
+    rest = fc(9)
+    for k, bit, sign in turned[1:]:
+        ts(fc(29), ic(k), sign, OP.mult, rest, OP.add)
+        rest = fc(29)
+    ts(v("zk"), v("zz"), fc(28), OP.add, rest, OP.add)
+    key = fc(10)
+    tt(key, fc(28), rest, OP.add)
     turn(v("rk"), v("zk"))
     quarters("rk", 0, 1)
     act(v("sgn"), v("rk"), AF.Sign, -1.0, key, fc(11))
@@ -350,58 +425,40 @@ def rank_program(g, core, T, topo):
     cp(v("pl", 0, 8), wp)
     pick("w0", "ws0", 0, 128, "q0", "q0s", 0, 128, v("pl", 0, 8))
 
-    peers = [(d, cores[r ^ d]) for d in range(1, N)]
-    chip = topo.cores_of(core)
-    far = [(d, c) for d, c in peers if c not in chip]
-    near = [(d, c) for d, c in peers if c in chip]
-    lanes = topo.engines(core, far[0][1])
-    spare = 2 * len(far) - len(lanes)
-    inside = [e for e in topo.engines(core, near[0][1]) if e not in lanes][:2]
-    ways = []
-    for part in range(2):
-        mine = lanes[spare:] + lanes[:spare] if part else lanes
-        way = {d: inside for d, c in near}
-        for k, (d, c) in enumerate(far):
-            way[d] = [mine[k]] if k < spare else [mine[spare + 2 * (k - spare)], mine[spare + 2 * (k - spare) + 1]]
-        ways.append(way)
-
-    def bits(es):
-        return sum(1 << e for e in es)
-
-    def dest(c):
-        rid, pid = topo.addr(c, core)
-        return DstId(rid=rid, pnc=pid)
-
-    def post(src, tr, leave, land):
+    def post(src, tr, leave, land, flight):
         def emit(e):
             order("G", [], [src])
             g.remote_dma_fused(tr, local_sem=T.sem.sent)
             total["sent"] = total.get("sent", 0) + leave
         i = add([], [src], emit, {"G": ISSUE})
-        add([land], [], None, {"R": 0.0}, FLIGHT, (i,))
+        add([land], [], None, {"R": 0.0}, flight, (i,))
 
-    def send(t, part):
-        name, dst = (("w" + t, "land" + t), ("ws" + t, "lands" + t))[part]
+    def send(part):
+        name, dst = (("w0", "ll"), ("ws0", "lls"))[part]
+        post(v(name, 0, 128), columns(name, dst, 0, 0, part, "arr0"), leave[part], v(dst, 16, 128), FLIGHT)
+
+    def send_merged(part):
+        if part == 0:
+            post(v("w0", 256, 384), columns("w0", "ll", 256, 128, 0, "arr1"), leave[0], v("ll", 144, 256), FLIGHT)
+        else:
+            tr = [RemoteDMATransfer(dst_ids=[dest(helper[core])], dma_engine_mask=bits(others), remote_sem=T.sem.hop,
+                                    src=T.ws0[:, 272:384], dst=T.hls[:, 16:128])]
+            post(v("ws0", 272, 384), tr, len(others), v("lls", 144, 256), FLIGHT + HOP)
+
+    def send_col(name, c0, dst, sem, flight):
         tr = []
-        for d, c in peers:
-            a, b = T[name][:, 16 * d:16 * d + 16], T[dst][:, 16 * d:16 * d + 16]
-            if part == 0:
-                a, b = a.bitcast(dt.uint8), b.bitcast(dt.uint8)
-            tr.append(RemoteDMATransfer(dst_ids=[dest(c)], dma_engine_mask=bits(ways[part][d]), remote_sem=T.sem["arr" + t], src=a, dst=b))
-        post(v(name, 0, 128), tr, sum(len(x) for x in ways[part].values()), v(dst, 16, 128))
-
-    def send_best(t):
-        c0, tr = 32 * int(t), []
         for who, es in ((far, lanes), (near, inside)):
-            tr.append(RemoteDMATransfer(dst_ids=[dest(c) for d, c in who], dma_engine_mask=bits(es), remote_sem=T.sem["thr" + t],
-                                        srcs=[T.mq[:, c0:c0 + 1]], dsts=[T["lt" + t][:, d:d + 1] for d, c in who]))
-        post(v("mq", c0, c0 + 1), tr, len(lanes) + len(inside), v("lt" + t, 1, 8))
+            tr.append(RemoteDMATransfer(dst_ids=[dest(c) for d, c in who], dma_engine_mask=bits(es), remote_sem=T.sem[sem],
+                                        srcs=[T[name][:, c0:c0 + 1]], dsts=[T[dst][:, d:d + 1] for d, c in who]))
+        post(v(name, c0, c0 + 1), tr, len(lanes) + len(inside), v(dst, 1, 8), flight)
 
-    for t in "01":
-        total["arr" + t] = sum(len(x) for w in ways for x in w.values())
-        total["thr" + t] = len(far) * len(lanes) + len(near) * len(inside)
-        note("R", [v("land" + t, 16, 128), v("lands" + t, 16, 128)], [], ("arr" + t, total["arr" + t]))
-        note("R", [v("lt" + t, 1, 8)], [], ("thr" + t, total["thr" + t]))
+    few = len(far) * len(lanes) + len(near) * len(inside)
+    for t in range(2):
+        total["arr%d" % t] = sum(leave)
+        note("R", [v("ll", 128 * t + 16, 128 * t + 128), v("lls", 128 * t + 16, 128 * t + 128)], [], ("arr%d" % t, total["arr%d" % t]))
+    for sem, dst in (("thr0", "lt0"), ("thr1", "lt1"), ("thd", "dt1")):
+        total[sem] = few
+        note("R", [v(dst, 1, 8)], [], (sem, few))
 
     def bank(k):
         return v("pm", 512 * k, 512 * k + 128)
@@ -416,13 +473,14 @@ def rank_program(g, core, T, topo):
                 act(x, x, AF.Identity, bias=v("pen1", col, col + 1), acc=out)
 
     def halves(t, k, part):
-        a = 128 * k
         if part == 0:
             m, s = v("w" + t, 0, 128), v("ws" + t, 0, 128)
         elif k == 2:
-            m, s = v("land" + t), v("lands" + t)
+            m, s = (v("l1"), v("l1s")) if t == "1" else (v("ll", 0, 128), v("lls", 0, 128))
+        elif t == "0":
+            m, s = v("gl"), v("gls")
         else:
-            m, s = v("g" + t, a, a + 128), v("gs" + t, a, a + 128)
+            m, s = v("g1", 128 * k, 128 * k + 128), v("gs1", 128 * k, 128 * k + 128)
         for b in range(4):
             mm(v("pn", 512 * b, 512 * b + 128), v("eq", 128 * b, 128 * b + 128), v("es", 128 * b, 128 * b + 128), m, s, part == 0, part == 1)
 
@@ -431,11 +489,12 @@ def rank_program(g, core, T, topo):
             cp(v("nt" + t, 512 * k + b, 512 * k + 512, 4), v("pn", 512 * b, 512 * b + 128), "VS")
 
     def requant(t, k):
-        a = 128 * k + 128
+        a = (256, 384, 128)[k]
         quant(v("w" + t, a, a + 128), v("ws" + t, a, a + 128), v("nt" + t, 512 * k, 512 * k + 512))
 
     for t in "01":
-        W, WS, G, GS, L, LS, sc, met = "w" + t, "ws" + t, "g" + t, "gs" + t, "land" + t, "lands" + t, "sc" + t, "met" + t
+        W, WS, G, GS, sc, met = "w" + t, "ws" + t, "g" + t, "gs" + t, "sc" + t, "met" + t
+        L, LS = ("ll", "lls") if t == "0" else ("l1", "l1s")
 
         def s_(a):
             return v(sc, a, a + 1)
@@ -445,8 +504,9 @@ def rank_program(g, core, T, topo):
 
         mb, mx = 32 * int(t), "mx" + t
         best = v("mq", mb, mb + 1)
-        send(t, 0)
-        send(t, 1)
+        if t == "0":
+            send(0)
+            send(1)
         mm(bank(0), v(W, 0, 128), v(WS, 0, 128), v(W, 0, 128), v(WS, 0, 128))
         if t == "0":
             ts(v("lf", 0, 24, 1, 0, 32), v("nl", 0, 72, 3, 0, 32), 0, OP.add)
@@ -465,21 +525,35 @@ def rank_program(g, core, T, topo):
             for k in range(2):
                 cp(v("xsl", 8 * k, 8 * k + 8), v("xs%d" % k, 15, 128, 16))
             ts(ic(4), ic(0), 1, OP.bitwise_and)
-            ts(ic(5), ic(0), 4, OP.arith_shift_right)
             ts(fc(13), ic(4), -2, OP.mult, fc(2), OP.add)
-            cp(fc(14), ic(5))
             ts(v("swl", 0, 1), fc(13), 1, OP.add)
             ts(v("dmb"), v("d24", 0, 8), fc(14), OP.not_equal, BIG, OP.mult)
+            ts(v("dmk"), v("d24", 0, 8), fc(14), OP.is_equal)
+            scores(t, [(0, 0, "e0", 0), (1, 0, "e1", 1)])
+            tt(best, s_(0), s_(1), OP.max)
+            tt(v("ed"), v("e1"), v("e0"), OP.subtract)
         else:
             ts(v("pen1", 0, 2), v("met0", 0, 2), -BIG / 128, OP.mult)
             ts(v("pen1", 4, 5), v("met0", 2, 3), -BIG / 128, OP.mult)
-        scores(t, [(0, 0, "e0", 0), (1, 0, "e1", 1)])
-        tt(best, s_(0), s_(1), OP.max)
-        send_best(t)
-        pick(G, GS, 0, 256, W, WS, 0, 128, v("xsl", 0, 16))
+            ts(fc(30), v("dsr", 0, 1), -BIG / 2, OP.mult, BIG, OP.add)
+            ts(fc(31), v("met0", 0, 1), v("met0", 1, 2), OP.subtract, BIG / 2, OP.mult)
+            act(v("nmA"), v("ed"), AF.Abs, fc(30), fc(31))
+            act(v("nm"), v("nmA"), AF.Identity, 1.0, -BIG)
+            tt(v("nmB"), bank(0), v("nm"), OP.add)
+            red(best, v("nmB"), OP.max)
+        send_col("mq", mb, "lt" + t, "thr" + t, (WAY0, WAY1)[int(t)])
+        if t == "0":
+            pick(G, GS, 0, 256, W, WS, 0, 128, v("xsl", 0, 16))
+            ts(fc(19), s_(1), s_(0), OP.is_gt)
+            wrap_sum("l", fc(19), fc(15), v("gll", 0, 8))
+            pick("gl", "gls", 0, 128, G, GS, 0, 256, v("gll", 0, 8))
+        else:
+            scores(t, [(0, 0, "e0", 0), (1, 0, "e1", 1)])
+            pick(G, GS, 0, 128, W, WS, 0, 128, v("xsl", 0, 8))
+            pick(G, GS, 128, 256, W, WS, 0, 128, v("xsl", 8, 16))
         halves(t, 0, 0)
         halves(t, 0, 1)
-        pick(L, LS, 0, 16, W, WS, 0, 128, v("swl", 0, 1))
+        pick("ll", "lls", 128 * int(t), 128 * int(t) + 16, W, WS, 0, 128, v("swl", 0, 1))
         mm(bank(2), v(G, 0, 128), v(GS, 0, 128), v(G, 128, 256), v(GS, 128, 256))
         mm(bank(3), v(G, 128, 256), v(GS, 128, 256), v(G, 0, 128), v(GS, 0, 128))
         if t == "1":
@@ -487,14 +561,20 @@ def rank_program(g, core, T, topo):
                 x = v("selm", 128 * k, 128 * k + 128)
                 choose(x, v("ks"), v("vl0"), v("e%d" % k))
                 act(x, x, AF.Copy, acc=fc(20 + k))
-            ts(v("pen1", 2, 3), fc(20), 2, OP.is_equal, -BIG / 128, OP.mult)
-            ts(v("pen1", 3, 4), fc(21), 1, OP.is_equal, -BIG / 128, OP.mult)
-            ts(v("pen1", 5, 7), v("fcol", 20, 22), 3, OP.is_equal, -BIG / 128, OP.mult)
+            ts(fc(22), v("sc0", 2, 3), v("sc0", 0, 1), OP.is_gt, -BIG / 128, OP.mult)
+            ts(fc(23), v("sc0", 3, 4), v("sc0", 1, 2), OP.is_ge, -BIG / 128, OP.mult)
+            ts(v("pen1", 2, 3), fc(20), 2, OP.is_equal, fc(22), OP.mult)
+            ts(v("pen1", 3, 4), fc(21), 2, OP.is_equal, fc(23), OP.mult)
+            ts(v("pen1", 5, 7), v("fcol", 20, 22), 1, OP.is_equal, -BIG / 128, OP.mult)
         drain(t, 0)
-        halves(t, 1, 0)
-        halves(t, 1, 1)
+        if t == "1":
+            halves(t, 1, 0)
+            halves(t, 1, 1)
         scores(t, [(2, 2, "e0", 2), (3, 3, "e1", 3)])
         requant(t, 0)
+        if t == "0":
+            send_merged(1)
+            send_merged(0)
         turn(v(mx, 0, 32, 1, 0, 32), v("mq", mb, mb + 32, 1, 0, 32))
         cp(v("mq", 64, 80, 2, 0, 32), v(mx, 1, 16, 2, 0, 32), "VS")
         cp(v("mq", 65, 80, 2, 0, 32), v(mx, 0, 16, 2, 0, 32), "VS")
@@ -504,48 +584,63 @@ def rank_program(g, core, T, topo):
         tt(s_(7), v("mq", 96, 97), best, OP.max)
         ts(s_(12), s_(10), -9 * BIG, OP.mult, s_(0), OP.add)
         ts(s_(13), s_(11), -9 * BIG, OP.mult, s_(1), OP.add)
-        drain(t, 1)
+        if t == "1":
+            drain(t, 1)
+            requant(t, 1)
         halves(t, 2, 0)
-        requant(t, 1)
         if t == "0":
             turn(v("lft", 0, 32, 1, 0, 32), v("lf", 0, 32, 1, 0, 32))
             dma("Y", "d_nbp", (v("nbp", 0, 384, 1, 0, 1), v("lft", 0, 16, 1, 0, 24)))
         else:
             ts(v("pl", 16, 24), wp, 256, OP.add)
-            tt(v("posm"), v("posn"), v("wm"), OP.mult)
-            gather(v("pa", 128, 512), v("nbp"), v("pl"), "VS")
-            scan(v("poss"), v("posm"))
-            ts(v("pol", 0, 8), v("poss", 15, 128, 16), -WHOLE, OP.add)
+            for k in range(2):
+                dma("Y", "d_pq%d" % k, (v("pq", 16 * k, 16 * k + 16, 1, 0, 8), v("posn", 0, 128, 1, 0, 1)))
+            turn(v("pqt", 0, 32, 1, 0, 32), v("pq", 0, 32, 1, 0, 32))
+            cp(v("pqt", 0, 8, 1, 32, 64), v("pqt", 0, 8, 1, 0, 32), "S")
+            cp(v("pqt", 0, 8, 1, 64, 128), v("pqt", 0, 8, 1, 0, 64), "S")
+            gather(v("pa", 128, 256), v("nbp"), v("pl", 16, 24), "VS")
+            gather(v("pa", 256, 512), v("nbp"), v("pl", 0, 16), "VS")
+            cp(v("pb", 128, 256), v("pa", 128, 256), "VS")
+            gather(v("pb", 256, 384), v("pa", 256, 512), v("gll", 0, 8), "VS")
+            ts(v("pol", 0, 8), v("pqt", 0, 8), -WHOLE, OP.add)
             quant(v("wq"), v("wqs"), v("wt", 0, 512))
-            gather(v("prs0"), v("pa"), v("vl0"), "VS")
+            gather(v("prs0"), v("pb"), v("vl0"), "VS")
             gather(v("pro0"), v("prs0"), v("pol", 0, 8), "VS")
             dma("Y", "d_p0", (T.pr[0:1, :], v("pro0", 0, 128, 1, 0, 1)))
-        mm(bank(0), v(W, 0, 128), v(WS, 0, 128), v(L), v(LS))
-        mm(bank(1), v(G, 0, 128), v(GS, 0, 128), v(L), v(LS))
-        mm(bank(2), v(G, 128, 256), v(GS, 128, 256), v(L), v(LS))
+            tt(v("dxm", 1, 8), v("dt1", 1, 8), v("dmk", 1, 8), OP.mult)
+            red(fc(24), v("dxm", 1, 8), OP.max)
+            wrap_sum("d", fc(24), fc(16), v("dll", 0, 8))
+            pick("l1", "l1s", 0, 128, "ll", "lls", 0, 256, v("dll", 0, 8))
+        l, ls = v(L, 0, 128), v(LS, 0, 128)
+        mm(bank(0), v(W, 0, 128), v(WS, 0, 128), l, ls)
+        mm(bank(1), v(G, 0, 128), v(GS, 0, 128), l, ls)
+        mm(bank(2), v(G, 128, 256), v(GS, 128, 256), l, ls)
         halves(t, 2, 1)
         scores(t, [(4, 0, "eye", 4), (5, 1, "e0", 5), (6, 2, "e1", 6)])
         ts(v("s4m" + t, 1, 8), v("dmb", 1, 8), s_(4), OP.add)
         ts(v("cq" + t, 0, 1), s_(7), s_(4), OP.is_lt)
         ts(m_(0), s_(5), s_(4), OP.max, s_(12), OP.is_le)
         ts(m_(1), s_(6), s_(4), OP.max, s_(13), OP.is_le)
-        ts(s_(15), m_(0), 128, OP.mult, fc(0), OP.add)
-        ts(s_(16), m_(1), 256, OP.mult, s_(15), OP.add)
+        if t == "0":
+            tt(v("dsr", 0, 1), m_(0), m_(1), OP.max)
+            send_col("dsr", 0, "dt1", "thd", HOP)
+        ts(s_(15), m_(0), 2, OP.mult, fc(15), OP.add)
+        ts(s_(16), m_(1), 2 + int(t), OP.mult, s_(15), OP.add)
         drain(t, 2)
         tt(v("cq" + t, 1, 8), v("lt" + t, 1, 8), v("s4m" + t, 1, 8), OP.is_lt)
         red(m_(2), v("cq" + t), OP.min)
-        ts(s_(18), m_(2), 384, OP.mult, s_(16), OP.add)
         requant(t, 2)
-        cp(v("vl" + t), wrap("v" + t, s_(18)))
+        wrap_sum("v" + t, m_(2), s_(16), v("vl" + t))
         if t == "0":
-            pick("w1", "ws1", 0, 128, W, WS, 0, 512, v("vl0"))
+            pick("w1", "ws1", 0, 128, W, WS, 0, 384, v("vl0"))
 
     pick("f0", "f0s", 0, 128, "w1", "ws1", 0, 512, v("vl1"))
-    pick("f1", "f1s", 0, 128, "f0", "f0s", 0, 128, v("pol", 0, 8))
+    last = pick("f1", "f1s", 0, 128, "f0", "f0s", 0, 128, v("pol", 0, 8))
     mm(bank(3), v("wq"), v("wqs"), v("f1"), v("f1s"))
     f1 = v("f1")
     dma("Y", "d_oc", (T.oc[:, :], (T.f1[:, :].bitcast(dt.uint8),) + f1[1:]))
     gather(v("prs1"), v("pa"), v("vl1"), "VS")
+    ops[-1][3].append(last)
     gather(v("pro1"), v("prs1"), v("pol", 0, 8), "VS")
     cp(v("yo"), bank(3), "VS")
     for k in range(4):

from concourse.bass import DstId, RemoteDMATransfer
from concourse.mybir import dt, AluOpType as OP, AxisListType, ActivationFunctionType as AF

F32, BF16, I32, U16, U8, C4 = "float32", "bfloat16", "int32", "uint16", "uint8", "float8_e4m3fn_x4"
SCRATCH = {"pn": ("psum", [128, 2048], F32), "pm": ("psum", [128, 2048], F32)}


def _declare(dtype, width, names):
    for n in names.split():
        SCRATCH[n] = ("sbuf", [128, width], dtype)


_declare(I32, 72, "nl")
_declare(I32, 16, "icol")
_declare(I32, 8, "nbt")
_declare(BF16, 520, "xt wt et")
_declare(BF16, 128, "sgn wmb wmh smb")
_declare(BF16, 8, "dmk dsr dt1 dxm")
_declare(F32, 64, "fcol")
_declare(F32, 24, "d24")
_declare(F32, 32, "lf lft pq pqt")
_declare(F32, 8, "dmb")
_declare(F32, 128, "mq npf npb n16 k128 wm nmA nmB nm ed zz sm eye zk rk zx rx dx e0 e1 posn yo xm0 xm1 xs0 xs1")
_declare(F32, 256, "selm npos nsl")
_declare(F32, 384, "nbp pb")
_declare(F32, 512, "ks pa")
_declare(U16, 24, "nlu pl swl cl xsl pol gll dll")
_declare(C4, 512, "eq")
_declare(U8, 512, "es")
_declare(C4, 256, "ll")
_declare(U8, 256, "lls")
_declare(U8, 128, "hls")
_declare(C4, 128, "q0 wq f0 f1 gl l1")
_declare(U8, 128, "q0s wqs f0s f1s gls l1s")
for _c in ("p", "v0", "v1", "l", "d"):
    _declare(BF16, 128, "qz%s qt%s qs%s" % (_c, _c, _c))
for _t in "01":
    _declare(C4, 512, "w" + _t)
    _declare(U8, 512, "ws" + _t)
    _declare(C4, 256, "g" + _t)
    _declare(U8, 256, "gs" + _t)
    _declare(F32, 8, "lt%s cq%s s4m%s pen%s met%s" % (_t, _t, _t, _t, _t))
    _declare(F32, 32, "mx%s sc%s" % (_t, _t))
    _declare(F32, 1024, "ex" + _t)
    _declare(BF16, 1536, "nt" + _t)
    _declare(U16, 8, "vl" + _t)
    _declare(F32, 128, "prs%s pro%s" % (_t, _t))
DMAS = ["d_nbt", "d_nbu", "d_n0", "d_n1", "d_n2", "d_x", "d_w", "d_nbp", "d_pq0", "d_pq1", "d_oc", "d_os0", "d_os1", "d_os2", "d_os3", "d_y", "d_p0", "d_p1"]
SEMAPHORES = ["cV", "cS", "cT", "cG", "sent", "arr0", "arr1", "thr0", "thr1", "thd", "hop"] + DMAS
BIG = 1e29
WAKE, TENS, LOAD, ISSUE, FLIGHT = 200.0, 130.0, 1000.0, 400.0, 3500.0
HOP, WAY0, WAY1 = 2500.0, 4200.0, 3000.0
LOOK = 250.0
WHOLE = 12582912.0


def rank_program(g, core, T, topo):
    N, cores = len(T.cores), T.cores
    owner, helper = {}, {}
    for c in cores:
        for h in topo.cores_of(c):
            if h not in cores and h not in owner and topo.die(h) == topo.die(c) and all(topo.may_write(h, d) for d in cores):
                owner[h], helper[c] = c, h
                break
    me = owner.get(core, core)
    r = T.rank_of(me)
    if r is None:
        return

    peers = [(d, cores[r ^ d]) for d in range(1, N)]
    chip = topo.cores_of(core)
    far = [(d, c) for d, c in peers if c not in chip]
    near = [(d, c) for d, c in peers if c in chip]
    lanes = topo.engines(core, far[0][1])
    spare = 2 * len(far) - len(lanes)
    others = [e for e in topo.engines(core, near[0][1]) if e not in lanes]
    inside = others[:2]
    ways = []
    for part in range(2):
        mine = lanes[spare:] + lanes[:spare] if part else lanes
        way = {d: inside for d, c in near}
        for k, (d, c) in enumerate(far):
            way[d] = [mine[k]] if k < spare else [mine[spare + 2 * (k - spare)], mine[spare + 2 * (k - spare) + 1]]
        ways.append(way)
    leave = [sum(len(x) for x in w.values()) for w in ways]

    def bits(es):
        return sum(1 << e for e in es)

    def dest(c):
        rid, pid = topo.addr(c, core)
        return DstId(rid=rid, pnc=pid)

    def columns(name, dst, c0, d0, part, sem):
        tr = []
        for d, c in peers:
            a, b = T[name][:, c0 + 16 * d:c0 + 16 * d + 16], T[dst][:, d0 + 16 * d:d0 + 16 * d + 16]
            if part == 0:
                a, b = a.bitcast(dt.uint8), b.bitcast(dt.uint8)
            tr.append(RemoteDMATransfer(dst_ids=[dest(c)], dma_engine_mask=bits(ways[part][d]), remote_sem=T.sem[sem], src=a, dst=b))
        return tr

    if core != me:
        g.wait_ge(T.sem.hop, len(others))
        g.remote_dma_fused(columns("hls", "lls", 0, 128, 1, "arr1"), local_sem=T.sem.sent)
        g.wait_ge(T.sem.sent, leave[1])
        return

    queue = {"V": g.vector, "S": g.scalar, "T": g.tensor, "G": g, "Y": g.sync}
    count = {e: 0 for e in "VSTG"}
    known = {e: {} for e in "VSTGY"}
    snap, hist, waited, total = {}, {}, {}, {}

    def v(name, c0=0, c1=None, st=1, p0=0, p1=128):
        c1 = SCRATCH[name][1][1] if c1 is None else c1
        ap = T[name][p0:p1, c0:c1] if st == 1 else T[name][p0:p1, c0:c1:st]
        if SCRATCH[name][0] == "psum":
            return (ap, name, 0, 128, c0 // 512 * 512, (c1 + 511) // 512 * 512, 1, 128)
        return (ap, name, p0, p1, c0, c1, st, (c1 - c0 + st - 1) // st)

    def meet(a, b):
        if a[3] <= b[2] or b[3] <= a[2] or a[5] <= b[4] or b[5] <= a[4]:
            return False
        return not (a[6] == b[6] and a[6] > 1 and (a[4] - b[4]) % a[6])

    def need(e, tok):
        sem, val = tok
        if known[e].get(sem, 0) < val:
            queue[e].wait_ge(T.sem[sem], val)
            waited[sem] = max(waited.get(sem, 0), val)
            for s, n in list(snap.get(tok, {}).items()) + [(sem, val)]:
                known[e][s] = max(known[e].get(s, 0), n)

    def order(e, outs, ins):
        toks = {}
        for x in ins:
            psum = SCRATCH[x[1]][0] == "psum"
            for (y, tok, w, f) in hist.get(x[1], []):
                if (w or (psum and f != e)) and meet(x, y):
                    toks[tok[0]] = max(toks.get(tok[0], 0), tok[1])
        for x in outs:
            for (y, tok, w, f) in hist.get(x[1], []):
                if (f != e or e != "T") and meet(x, y):
                    toks[tok[0]] = max(toks.get(tok[0], 0), tok[1])
        for s in sorted(toks, key=lambda s: s == "c" + e):
            need(e, (s, toks[s]))

    def note(e, outs, ins, tok):
        for x in outs:
            hist.setdefault(x[1], []).append((x, tok, True, e))
        for x in ins:
            hist.setdefault(x[1], []).append((x, tok, False, e))

    ops, seen = [], {}

    def views(xs):
        return [x for x in xs if isinstance(x, tuple)]

    def add(outs, ins, emit, cost, late=0.0, after=()):
        e, outs, ins = "".join(cost), views(outs), views(ins)
        i, deps = len(ops), set(after)
        for x in ins:
            psum = SCRATCH[x[1]][0] == "psum"
            deps.update(j for y, j, w, f in seen.get(x[1], []) if (w or (psum and f != e)) and meet(x, y))
        for x in outs:
            deps.update(j for y, j, w, f in seen.get(x[1], []) if meet(x, y))
        for x in outs:
            seen.setdefault(x[1], []).append((x, i, True, e))
        for x in ins:
            seen.setdefault(x[1], []).append((x, i, False, e))
        ops.append((emit, cost, late, sorted(deps)))
        return i

    def run(outs, ins, call, cost):
        outs, ins = views(outs), views(ins)

        def emit(e):
            order(e, outs, ins)
            count[e] += 1
            tok = ("c" + e, count[e])
            call(e).then_inc(T.sem[tok[0]], 1)
            total[tok[0]] = count[e]
            snap[tok] = dict(known[e])
            note(e, outs, ins, tok)
        return add(outs, ins, emit, cost)

    def schedule():
        n = len(ops)
        users = [[] for _ in ops]
        for i, o in enumerate(ops):
            for j in o[3]:
                users[j].append(i)
        way = [0.0] * n
        for i in range(n - 1, -1, -1):
            way[i] = min(ops[i][1].values()) + ops[i][2] + max([way[j] + WAKE for j in users[i]] + [0.0])
        left, end, free = [len(o[3]) for o in ops], [0.0] * n, {}
        ready = {i: 0.0 for i in range(n) if not left[i]}
        when = []
        while ready:
            best = None
            for e in "RVSTGY":
                c = [(s, i) for i, s in ready.items() if e in ops[i][1]]
                if not c:
                    continue
                t = free.get(e, 0.0)
                if e == "R":
                    x, t = min(c), 0.0
                elif e == "G":
                    x = min(c, key=lambda y: y[1])
                else:
                    t0 = max(t, min(c)[0])
                    x = max([y for y in c if y[0] <= t0 + LOOK], key=lambda y: (way[y[1]] - max(0.0, y[0] - t0), -y[1]))
                    if x[0] > t0:
                        fit = [y for y in c if max(t, y[0]) + ops[y[1]][1][e] <= x[0]]
                        if fit:
                            x = max(fit, key=lambda y: (way[y[1]], -y[1]))
                s = max(t, x[0])
                z = s + ops[x[1]][1][e]
                if best is None or (s, z) < best[:2]:
                    best = (s, z, e, x[1])
            s, z, e, i = best
            end[i] = z + ops[i][2]
            free[e] = z
            when.append((s, len(when), e, i))
            del ready[i]
            for j in users[i]:
                left[j] -= 1
                if not left[j]:
                    ready[j] = max(end[m] for m in ops[j][3]) + WAKE
        for s, k, e, i in when:
            if e != "R":
                ops[i][0](e)

    def val(x):
        return x[0] if isinstance(x, tuple) else x

    def dma(e, sem, *moves):
        outs, ins = views([x for x, y in moves]), views([y for x, y in moves])

        def emit(e):
            for out, in_ in moves:
                order(e, views([out]), views([in_]))
                queue[e].dma_start(val(out), val(in_)).then_inc(T.sem[sem], 16)
            total[sem] = 16 * len(moves)
            snap[(sem, total[sem])] = dict(known[e])
            note("D" + sem, outs, ins, (sem, total[sem]))
        add(outs, ins, emit, {e: 60.0 * len(moves)}, LOAD)

    def vec(x, a=1.0):
        return max(64, a * x[7] * (0.5 if SCRATCH[x[1]][2] == BF16 else 1)) * 0.83

    def ts(out, a, s1, op0, s2=None, op1=None):
        if op1 is None:
            run([out], [a, s1], lambda e: g.vector.tensor_scalar(out[0], a[0], val(s1), None, op0), {"V": vec(a)})
        else:
            run([out], [a, s1, s2], lambda e: g.vector.tensor_scalar(out[0], a[0], val(s1), val(s2), op0, op1), {"V": vec(a)})

    def tt(out, a, b, op):
        run([out], [a, b], lambda e: g.vector.tensor_tensor(out[0], a[0], b[0], op), {"V": vec(a, 1 if a[1] in ("pn", "pm") else 2)})

    def act(out, a, func, scale=1.0, bias=0.0, acc=None):
        if acc is None:
            run([out], [a, bias, scale], lambda e: g.scalar.activation(out[0], a[0], func, bias=val(bias), scale=val(scale)), {"S": vec(a)})
        else:
            run([out, acc], [a, bias], lambda e: g.scalar.activation(out[0], a[0], func, bias=val(bias), scale=scale, accum_out=acc[0]), {"S": vec(a) + 20})

    def cp(out, a, es="V"):
        def call(e):
            if e == "V":
                return g.vector.tensor_copy(out[0], a[0])
            return g.scalar.activation(out[0], a[0], AF.Copy)
        run([out], [a], call, {e: vec(a) for e in es})

    def fill(out, c):
        run([out], [], lambda e: g.vector.memset(out[0], c), {"V": vec(out)})

    def red(out, a, op, ab=False):
        run([out], [a], lambda e: g.vector.tensor_reduce(out[0], a[0], AxisListType.X, op, apply_absolute_value=ab), {"V": vec(a)})

    def turn(out, a):
        run([out], [a], lambda e: g.vector.transpose(out[0], a[0]), {"V": vec(a)})

    def scan(z, q, op=OP.add):
        s = v("smb" if SCRATCH[q[1]][2] == BF16 else "sm")
        run([z], [q, s], lambda e: g.vector.tensor_tensor_scan(z[0], s[0], q[0], 0.0, OP.mult, op), {"V": vec(q)})

    def quant(q, s, a):
        run([q, s], [a], lambda e: g.vector.quantize_mx(q[0], s[0], a[0]), {"V": 12 + 0.22 * a[7]})

    def mm(out, a, asc, b, bsc, start=True, stop=True):
        run([out], [a, asc, b, bsc], lambda e: g.tensor.matmul_mx(out[0], a[0], asc[0], b[0], bsc[0], start, stop), {"T": TENS})

    def by_list(out):
        return 60 + 1.25 * out[7]

    def gather(out, win, off, es="S", func=AF.Copy, scale=1.0, bias=0.0):
        def call(e):
            if e == "V":
                return g.vector.tensor_copy(out[0], win[0].indirect(off[0]))
            if func == AF.Copy:
                return g.scalar.activation(out[0], win[0].indirect(off[0]), AF.Copy)
            return g.scalar.activation(out[0], win[0].indirect(off[0]), func, bias=bias, scale=scale)
        run([out], [win, off], call, {e: by_list(out) for e in es})

    def choose(out, win, off, m):
        run([out], [win, off, m], lambda e: g.vector.tensor_tensor(out[0], win[0].indirect(off[0]), m[0], OP.mult), {"V": by_list(out)})

    def pick(oq, os, oa, ob, iq, isc, ia, ib, off):
        o, w = v(oq, oa, ob), v(iq, ia, ib)
        i = run([o], [w, off], lambda e: g.vector.tensor_copy(o[0].bitcast(dt.uint32), w[0].bitcast(dt.uint32).indirect(off[0])), {"V": by_list(o)})
        gather(v(os, oa, ob), v(isc, ia, ib), off)
        return i

    def iota(out, pattern, base, cm, flag=True):
        run([out], [], lambda e: g.iota(out[0], pattern, base, cm, allow_small_or_imprecise_dtypes=True) if flag else g.iota(out[0], pattern, base, cm),
            {"G": 130 + 1.66 * out[7]})

    def quarters(name, c0, st):
        for d in range(4):
            a = d ^ 1
            cp(v(name, 32 * a + c0, 32 * a + 32, st, 32 * d, 32 * d + 32), v(name, 32 * a + c0, 32 * a + 32, st, 32 * a, 32 * a + 32), "VS")
        cp(v(name, 64 + c0, 128, st, 0, 64), v(name, 64 + c0, 128, st, 64, 128), "VS")
        cp(v(name, c0, 64, st, 64, 128), v(name, c0, 64, st, 0, 64), "VS")

    def wrap(tag, col):
        ts(v("qz" + tag), v("wmh"), col, OP.mult)
        turn(v("qt" + tag), v("qz" + tag))
        scan(v("qs" + tag), v("qt" + tag))
        quarters("qs" + tag, 15, 16)
        return v("qs" + tag, 15, 128, 16)

    def wrap_sum(tag, a, b, out):
        ts(v("qz" + tag), v("wmb"), a, OP.add, b, OP.add)
        turn(v("qt" + tag), v("qz" + tag))
        scan(v("qs" + tag), v("qt" + tag), OP.max)
        quarters("qs" + tag, 15, 16)
        ts(out, v("qs" + tag, 15, 128, 16), 128, OP.mult, fc(17), OP.add)

    def ic(k):
        return v("icol", k, k + 1)

    def fc(k):
        return v("fcol", k, k + 1)

    classes = ((2, 0, 5), (1, 5, 5), (0, 10, 6))
    part = [(v("nbt", 2 - (2 - i) % 3, 5 - (2 - i) % 3, 1, 8 * s, 8 * (s + n)), T.nb[i:16:3, :]) for i, s, n in classes]
    dma("S", "d_nbu", part[0])
    dma("Y", "d_nbt", *part[1:])
    dma("S", "d_x", (v("xt", 0, 512), T.x[:, :]))
    for k, by in ((0, 6), (1, 11), (2, 0)):
        moves = []
        for h in range(2):
            for i, s, n in classes:
                p, c = 16 * h + (s + by) % 16, (k - i) % 3
                moves.append((v("nl", 24 * k, 24 * k + 22, 1, p, p + n), T.nb[i:16:3, c:c + 22]))
        dma("Y", "d_n%d" % k, *moves)
    dma("Y", "d_w", (v("wt", 0, 512), T.w[:, :]))

    iota(ic(0), [[0, 1]], 0, 1, False)
    iota(v("npf"), [[1, 128]], 0, -1)
    iota(v("k128"), [[0, 128]], 128, 0)
    iota(v("n16"), [[0, 8], [1, 16]], 0, 0)
    iota(fc(0), [[0, 1]], 0, 1)
    iota(v("d24"), [[1, 24]], 0, 0)
    iota(fc(6), [[0, 1]], -64, 256)
    iota(v("lf"), [[0, 32]], 0, 0)
    iota(v("ks"), [[1, 4], [0, 128]], 0, 0)
    iota(v("nbp"), [[0, 384]], 0, 0)
    iota(v("pa", 0, 128), [[0, 128]], -1, 0)
    iota(v("pb", 0, 128), [[0, 128]], -1, 0)
    fill(v("zz"), 0.0)
    fill(v("et"), 0.0)
    fill(v("mq"), -BIG)
    ts(ic(1), ic(0), 3, OP.arith_shift_right)
    ts(ic(2), ic(0), 7, OP.bitwise_and)
    ts(ic(3), ic(0), 15, OP.bitwise_and)
    cp(fc(1), ic(1))
    cp(fc(2), ic(3))
    ts(fc(3), ic(2), 16, OP.mult, fc(1), OP.add)
    ts(fc(7), fc(2), 8, OP.mult)
    ts(fc(4), fc(3), 128 * r, OP.add)
    ts(fc(5), fc(3), 128 * 127 - 64, OP.add)
    act(v("npb"), v("npf"), AF.Abs)
    act(v("eye"), v("npb"), AF.Relu, -1.0, 1.0)
    act(v("et", 4, 516, 4), v("eye"), AF.Copy, 0.5)
    for b in range(4):
        quant(v("eq", 128 * b, 128 * b + 128), v("es", 128 * b, 128 * b + 128), v("et", 4 - b, 516 - b))
    act(v("sm"), v("n16"), AF.Sign)
    ts(v("wm"), v("n16"), fc(2), OP.is_equal)
    ts(v("wmb"), v("n16"), fc(2), OP.is_equal, 4, OP.mult)
    ts(v("wmh"), v("n16"), fc(2), OP.is_equal)
    cp(v("smb"), v("sm"), "S")
    ts(ic(5), ic(0), 4, OP.arith_shift_right)
    cp(fc(14), ic(5))
    ts(fc(15), fc(14), 0.125, OP.mult)
    ts(fc(16), fc(14), 0, OP.is_equal, fc(15), OP.add)
    ts(fc(17), fc(2), -512, OP.add)
    fill(v("pq", 0, 32, 1, 0, 32), 0.0)

    ts(fc(9), v("nbt", 2, 3), 0.5, OP.add, fc(4), OP.min)
    turned = [(k, bit, sign) for k, bit, sign in ((8, 128 * r, -8), (9, 896 - 128 * r, 8)) if bit]
    for k, bit, sign in turned:
        ts(ic(k), v("nbt", 2, 3), bit, OP.bitwise_and)
    k, bit, sign = turned[0]
    ts(fc(28), ic(k), sign, OP.mult)
    rest = fc(9)
    for k, bit, sign in turned[1:]:
        ts(fc(29), ic(k), sign, OP.mult, rest, OP.add)
        rest = fc(29)
    ts(v("zk"), v("zz"), fc(28), OP.add, rest, OP.add)
    key = fc(10)
    tt(key, fc(28), rest, OP.add)
    turn(v("rk"), v("zk"))
    quarters("rk", 0, 1)
    act(v("sgn"), v("rk"), AF.Sign, -1.0, key, fc(11))
    ts(v("cl", 0, 8), v("d24", 0, 8), fc(7), OP.add)
    quant(v("q0"), v("q0s"), v("xt", 0, 512))
    ts(v("zx"), v("k128"), fc(11), OP.mult, fc(5), OP.add)
    turn(v("rx"), v("zx"))
    quarters("rx", 0, 1)
    ts(v("dx"), v("rx"), fc(6), OP.subtract)
    red(fc(12), v("dx"), OP.min, True)
    gather(v("posn"), v("rx"), v("cl", 0, 8), "S", AF.Identity, 1.0 / 256, WHOLE)
    wp = wrap("p", fc(12))
    cp(v("pl", 0, 8), wp)
    pick("w0", "ws0", 0, 128, "q0", "q0s", 0, 128, v("pl", 0, 8))

    def post(src, tr, leave, land, flight):
        def emit(e):
            order("G", [], [src])
            g.remote_dma_fused(tr, local_sem=T.sem.sent)
            total["sent"] = total.get("sent", 0) + leave
        i = add([], [src], emit, {"G": ISSUE})
        add([land], [], None, {"R": 0.0}, flight, (i,))

    def send(part):
        name, dst = (("w0", "ll"), ("ws0", "lls"))[part]
        post(v(name, 0, 128), columns(name, dst, 0, 0, part, "arr0"), leave[part], v(dst, 16, 128), FLIGHT)

    def send_merged(part):
        if part == 0:
            post(v("w0", 256, 384), columns("w0", "ll", 256, 128, 0, "arr1"), leave[0], v("ll", 144, 256), FLIGHT)
        else:
            tr = [RemoteDMATransfer(dst_ids=[dest(helper[core])], dma_engine_mask=bits(others), remote_sem=T.sem.hop,
                                    src=T.ws0[:, 272:384], dst=T.hls[:, 16:128])]
            post(v("ws0", 272, 384), tr, len(others), v("lls", 144, 256), FLIGHT + HOP)

    def send_col(name, c0, dst, sem, flight):
        tr = []
        for who, es in ((far, lanes), (near, inside)):
            tr.append(RemoteDMATransfer(dst_ids=[dest(c) for d, c in who], dma_engine_mask=bits(es), remote_sem=T.sem[sem],
                                        srcs=[T[name][:, c0:c0 + 1]], dsts=[T[dst][:, d:d + 1] for d, c in who]))
        post(v(name, c0, c0 + 1), tr, len(lanes) + len(inside), v(dst, 1, 8), flight)

    few = len(far) * len(lanes) + len(near) * len(inside)
    for t in range(2):
        total["arr%d" % t] = sum(leave)
        note("R", [v("ll", 128 * t + 16, 128 * t + 128), v("lls", 128 * t + 16, 128 * t + 128)], [], ("arr%d" % t, total["arr%d" % t]))
    for sem, dst in (("thr0", "lt0"), ("thr1", "lt1"), ("thd", "dt1")):
        total[sem] = few
        note("R", [v(dst, 1, 8)], [], (sem, few))

    def bank(k):
        return v("pm", 512 * k, 512 * k + 128)

    def scores(t, jobs):
        for k, b, m, col in jobs:
            x, out = v("ex" + t, 128 * k, 128 * k + 128), v("sc" + t, col, col + 1)
            tt(x, bank(b), v(m), OP.mult)
            if t == "0":
                act(x, x, AF.Copy, acc=out)
            else:
                act(x, x, AF.Identity, bias=v("pen1", col, col + 1), acc=out)

    def halves(t, k, part):
        if part == 0:
            m, s = v("w" + t, 0, 128), v("ws" + t, 0, 128)
        elif k == 2:
            m, s = (v("l1"), v("l1s")) if t == "1" else (v("ll", 0, 128), v("lls", 0, 128))
        elif t == "0":
            m, s = v("gl"), v("gls")
        else:
            m, s = v("g1", 128 * k, 128 * k + 128), v("gs1", 128 * k, 128 * k + 128)
        for b in range(4):
            mm(v("pn", 512 * b, 512 * b + 128), v("eq", 128 * b, 128 * b + 128), v("es", 128 * b, 128 * b + 128), m, s, part == 0, part == 1)

    def drain(t, k):
        for b in range(4):
            cp(v("nt" + t, 512 * k + b, 512 * k + 512, 4), v("pn", 512 * b, 512 * b + 128), "VS")

    def requant(t, k):
        a = (256, 384, 128)[k]
        quant(v("w" + t, a, a + 128), v("ws" + t, a, a + 128), v("nt" + t, 512 * k, 512 * k + 512))

    for t in "01":
        W, WS, G, GS, sc, met = "w" + t, "ws" + t, "g" + t, "gs" + t, "sc" + t, "met" + t
        L, LS = ("ll", "lls") if t == "0" else ("l1", "l1s")

        def s_(a):
            return v(sc, a, a + 1)

        def m_(a):
            return v(met, a, a + 1)

        mb, mx = 32 * int(t), "mx" + t
        best = v("mq", mb, mb + 1)
        if t == "0":
            send(0)
            send(1)
        mm(bank(0), v(W, 0, 128), v(WS, 0, 128), v(W, 0, 128), v(WS, 0, 128))
        if t == "0":
            ts(v("lf", 0, 24, 1, 0, 32), v("nl", 0, 72, 3, 0, 32), 0, OP.add)
            cp(v("lf", 0, 16, 1, 32, 64), v("lf", 0, 16, 1, 0, 32), "S")
            cp(v("lf", 0, 16, 1, 64, 128), v("lf", 0, 16, 1, 0, 64), "S")
            ts(v("nlu", 0, 16), v("lf", 0, 16), -128 * r, OP.add)
            gather(v("npos"), v("posn"), v("nlu", 0, 16), "S", AF.Identity, 1.0, -WHOLE)
            ts(v("pl", 8, 16), wp, 128, OP.add)
            gather(v("nsl"), v("npos"), v("pl", 0, 16))
            for k in range(2):
                ts(v("e%d" % k), v("nsl", 128 * k, 128 * k + 128), fc(0), OP.is_equal)
            for k in range(2):
                choose(v("xm%d" % k), v("npos", 128 * k, 128 * k + 128), v("pl", 0, 8), v("wm"))
            for k in range(2):
                scan(v("xs%d" % k), v("xm%d" % k))
            for k in range(2):
                cp(v("xsl", 8 * k, 8 * k + 8), v("xs%d" % k, 15, 128, 16))
            ts(ic(4), ic(0), 1, OP.bitwise_and)
            ts(fc(13), ic(4), -2, OP.mult, fc(2), OP.add)
            ts(v("swl", 0, 1), fc(13), 1, OP.add)
            ts(v("dmb"), v("d24", 0, 8), fc(14), OP.not_equal, BIG, OP.mult)
            ts(v("dmk"), v("d24", 0, 8), fc(14), OP.is_equal)
            scores(t, [(0, 0, "e0", 0), (1, 0, "e1", 1)])
            tt(best, s_(0), s_(1), OP.max)
            tt(v("ed"), v("e1"), v("e0"), OP.subtract)
        else:
            ts(v("pen1", 0, 2), v("met0", 0, 2), -BIG / 128, OP.mult)
            ts(v("pen1", 4, 5), v("met0", 2, 3), -BIG / 128, OP.mult)
            ts(fc(30), v("dsr", 0, 1), -BIG / 2, OP.mult, BIG, OP.add)
            ts(fc(31), v("met0", 0, 1), v("met0", 1, 2), OP.subtract, BIG / 2, OP.mult)
            act(v("nmA"), v("ed"), AF.Abs, fc(30), fc(31))
            act(v("nm"), v("nmA"), AF.Identity, 1.0, -BIG)
            tt(v("nmB"), bank(0), v("nm"), OP.add)
            red(best, v("nmB"), OP.max)
        send_col("mq", mb, "lt" + t, "thr" + t, (WAY0, WAY1)[int(t)])
        if t == "0":
            pick(G, GS, 0, 256, W, WS, 0, 128, v("xsl", 0, 16))
            ts(fc(19), s_(1), s_(0), OP.is_gt)
            wrap_sum("l", fc(19), fc(15), v("gll", 0, 8))
            pick("gl", "gls", 0, 128, G, GS, 0, 256, v("gll", 0, 8))
        else:
            scores(t, [(0, 0, "e0", 0), (1, 0, "e1", 1)])
            pick(G, GS, 0, 128, W, WS, 0, 128, v("xsl", 0, 8))
            pick(G, GS, 128, 256, W, WS, 0, 128, v("xsl", 8, 16))
        halves(t, 0, 0)
        halves(t, 0, 1)
        pick("ll", "lls", 128 * int(t), 128 * int(t) + 16, W, WS, 0, 128, v("swl", 0, 1))
        mm(bank(2), v(G, 0, 128), v(GS, 0, 128), v(G, 128, 256), v(GS, 128, 256))
        mm(bank(3), v(G, 128, 256), v(GS, 128, 256), v(G, 0, 128), v(GS, 0, 128))
        if t == "1":
            for k in range(2):
                x = v("selm", 128 * k, 128 * k + 128)
                choose(x, v("ks"), v("vl0"), v("e%d" % k))
                act(x, x, AF.Copy, acc=fc(20 + k))
            ts(fc(22), v("sc0", 2, 3), v("sc0", 0, 1), OP.is_gt, -BIG / 128, OP.mult)
            ts(fc(23), v("sc0", 3, 4), v("sc0", 1, 2), OP.is_ge, -BIG / 128, OP.mult)
            ts(v("pen1", 2, 3), fc(20), 2, OP.is_equal, fc(22), OP.mult)
            ts(v("pen1", 3, 4), fc(21), 2, OP.is_equal, fc(23), OP.mult)
            ts(v("pen1", 5, 7), v("fcol", 20, 22), 1, OP.is_equal, -BIG / 128, OP.mult)
        drain(t, 0)
        if t == "1":
            halves(t, 1, 0)
            halves(t, 1, 1)
        scores(t, [(2, 2, "e0", 2), (3, 3, "e1", 3)])
        requant(t, 0)
        if t == "0":
            send_merged(1)
            send_merged(0)
        turn(v(mx, 0, 32, 1, 0, 32), v("mq", mb, mb + 32, 1, 0, 32))
        cp(v("mq", 64, 80, 2, 0, 32), v(mx, 1, 16, 2, 0, 32), "VS")
        cp(v("mq", 65, 80, 2, 0, 32), v(mx, 0, 16, 2, 0, 32), "VS")
        turn(v("mq", 96, 128, 1, 0, 32), v("mq", 64, 96, 1, 0, 32))
        ts(s_(10), s_(1), s_(2), OP.max, s_(0), OP.is_gt)
        ts(s_(11), s_(0), s_(3), OP.max, s_(1), OP.is_ge)
        tt(s_(7), v("mq", 96, 97), best, OP.max)
        ts(s_(12), s_(10), -9 * BIG, OP.mult, s_(0), OP.add)
        ts(s_(13), s_(11), -9 * BIG, OP.mult, s_(1), OP.add)
        if t == "1":
            drain(t, 1)
            requant(t, 1)
        halves(t, 2, 0)
        if t == "0":
            turn(v("lft", 0, 32, 1, 0, 32), v("lf", 0, 32, 1, 0, 32))
            dma("Y", "d_nbp", (v("nbp", 0, 384, 1, 0, 1), v("lft", 0, 16, 1, 0, 24)))
        else:
            ts(v("pl", 16, 24), wp, 256, OP.add)
            for k in range(2):
                dma("Y", "d_pq%d" % k, (v("pq", 16 * k, 16 * k + 16, 1, 0, 8), v("posn", 0, 128, 1, 0, 1)))
            turn(v("pqt", 0, 32, 1, 0, 32), v("pq", 0, 32, 1, 0, 32))
            cp(v("pqt", 0, 8, 1, 32, 64), v("pqt", 0, 8, 1, 0, 32), "S")
            cp(v("pqt", 0, 8, 1, 64, 128), v("pqt", 0, 8, 1, 0, 64), "S")
            gather(v("pa", 128, 256), v("nbp"), v("pl", 16, 24), "VS")
            gather(v("pa", 256, 512), v("nbp"), v("pl", 0, 16), "VS")
            cp(v("pb", 128, 256), v("pa", 128, 256), "VS")
            gather(v("pb", 256, 384), v("pa", 256, 512), v("gll", 0, 8), "VS")
            ts(v("pol", 0, 8), v("pqt", 0, 8), -WHOLE, OP.add)
            quant(v("wq"), v("wqs"), v("wt", 0, 512))
            gather(v("prs0"), v("pb"), v("vl0"), "VS")
            gather(v("pro0"), v("prs0"), v("pol", 0, 8), "VS")
            dma("Y", "d_p0", (T.pr[0:1, :], v("pro0", 0, 128, 1, 0, 1)))
            tt(v("dxm", 1, 8), v("dt1", 1, 8), v("dmk", 1, 8), OP.mult)
            red(fc(24), v("dxm", 1, 8), OP.max)
            wrap_sum("d", fc(24), fc(16), v("dll", 0, 8))
            pick("l1", "l1s", 0, 128, "ll", "lls", 0, 256, v("dll", 0, 8))
        l, ls = v(L, 0, 128), v(LS, 0, 128)
        mm(bank(0), v(W, 0, 128), v(WS, 0, 128), l, ls)
        mm(bank(1), v(G, 0, 128), v(GS, 0, 128), l, ls)
        mm(bank(2), v(G, 128, 256), v(GS, 128, 256), l, ls)
        halves(t, 2, 1)
        scores(t, [(4, 0, "eye", 4), (5, 1, "e0", 5), (6, 2, "e1", 6)])
        ts(v("s4m" + t, 1, 8), v("dmb", 1, 8), s_(4), OP.add)
        ts(v("cq" + t, 0, 1), s_(7), s_(4), OP.is_lt)
        ts(m_(0), s_(5), s_(4), OP.max, s_(12), OP.is_le)
        ts(m_(1), s_(6), s_(4), OP.max, s_(13), OP.is_le)
        if t == "0":
            tt(v("dsr", 0, 1), m_(0), m_(1), OP.max)
            send_col("dsr", 0, "dt1", "thd", HOP)
        ts(s_(15), m_(0), 2, OP.mult, fc(15), OP.add)
        ts(s_(16), m_(1), 2 + int(t), OP.mult, s_(15), OP.add)
        drain(t, 2)
        tt(v("cq" + t, 1, 8), v("lt" + t, 1, 8), v("s4m" + t, 1, 8), OP.is_lt)
        red(m_(2), v("cq" + t), OP.min)
        requant(t, 2)
        wrap_sum("v" + t, m_(2), s_(16), v("vl" + t))
        if t == "0":
            pick("w1", "ws1", 0, 128, W, WS, 0, 384, v("vl0"))

    pick("f0", "f0s", 0, 128, "w1", "ws1", 0, 512, v("vl1"))
    last = pick("f1", "f1s", 0, 128, "f0", "f0s", 0, 128, v("pol", 0, 8))
    mm(bank(3), v("wq"), v("wqs"), v("f1"), v("f1s"))
    f1 = v("f1")
    dma("Y", "d_oc", (T.oc[:, :], (T.f1[:, :].bitcast(dt.uint8),) + f1[1:]))
    gather(v("prs1"), v("pa"), v("vl1"), "VS")
    ops[-1][3].append(last)
    gather(v("pro1"), v("prs1"), v("pol", 0, 8), "VS")
    cp(v("yo"), bank(3), "VS")
    for k in range(4):
        dma("Y", "d_os%d" % k, (T.osc[4 * k:4 * k + 4, :], v("f1s", 0, 128, 1, 32 * k, 32 * k + 4)))
    dma("S", "d_y", (T.y[:, :], v("yo")))
    dma("Y", "d_p1", (T.pr[1:2, :], v("pro1", 0, 128, 1, 0, 1)))
    schedule()
    for sem, n in total.items():
        if waited.get(sem, 0) < n:
            (g if sem == "sent" else g.sync).wait_ge(T.sem[sem], n)
